import numpy as np
import ml_dtypes


def mxq(x, axis, fmt="e4m3"):
    dtype, down = {"e4m3": (ml_dtypes.float8_e4m3fn, 7), "e5m2": (ml_dtypes.float8_e5m2, 14)}[fmt]
    v = np.moveaxis(np.asarray(x, np.float32).astype(ml_dtypes.bfloat16).astype(np.float64), axis, -1)
    blocks = v.reshape(v.shape[:-1] + (-1, 32))
    amax = np.abs(blocks).max(-1, keepdims=True)
    byte = np.maximum(np.where(amax > 0, np.frexp(amax)[1] - 1 + 127, 0) - down, 1)
    scale = np.exp2(byte - 127.0)
    codes = (blocks / scale).astype(np.float32).astype(dtype).astype(np.float64)
    return np.moveaxis((codes * scale).reshape(v.shape), -1, axis)


WIDE = False


def mx_kscale(k):
    if not WIDE:
        return np.ones(k)
    levels = np.array([10, -10, 5, -5, 0])
    if k % 512:
        return np.exp2(np.random.permutation(np.resize(levels, k // 32))).repeat(32)
    a = np.empty((k // 512, 16))
    for p in range(k // 512):
        a[p, :8] = np.random.permutation(np.resize(levels, 8))
        for g in range(8):
            far = levels[np.abs(levels - a[p, g]) >= 10]
            a[p, g + 8] = far[np.random.randint(len(far))]
    return np.exp2(a.ravel()).repeat(32)


def f64(x):
    return np.asarray(x).astype(np.float64)


def striped(idx):
    return np.tile(np.asarray(idx).reshape(-1, 16).T, (8, 1)).astype(np.uint16)


def unstriped(offs):
    return offs[:16].T.reshape(-1).astype(np.int64)


G, K, T, D, M = 512, 2, 4096, 512, 512


def setup_inputs():
    n = np.random.standard_normal
    s = mx_kscale(D)[:, None]
    grid = lambda x: np.round(x * 32) / 32
    x = grid(n((D, T))) * s
    idx = np.random.randint(0, T, (G, K))
    return {
        "xT": x.astype(np.float32),
        "w": (n((D, M)) / np.sqrt(D * K) / s).astype(np.float32),
        "bias": (0.3 * n((M, 1))).astype(np.float32),
        "offs": striped(idx.reshape(-1)),
    }


def reference(xT, w, bias, offs):
    x = f64(xT)[:, unstriped(offs)]
    y = mxq(f64(w), 0, "e4m3").T @ mxq(x.reshape(D, G, K).sum(-1), 0, "e4m3")
    y = y + f64(bias)
    return y

@@ -1,0 +1,124 @@
+from contextlib import ExitStack
+
+import concourse.mybir as mybir
+
+D, T, G, BAG, M = 512, 4096, 512, 2, 512
+FLOPS = 2 * D * M * G
+
+F32 = mybir.dt.float32
+BF16 = mybir.dt.bfloat16
+U32 = mybir.dt.uint32
+U16 = mybir.dt.uint16
+U8 = mybir.dt.uint8
+FP8X4 = mybir.dt.float8_e4m3fn_x4
+ADD = mybir.AluOpType.add
+IDENTITY = mybir.ActivationFunctionType.Identity
+
+P = 128
+PACK = 4
+HALVES = 2
+G_HALF = G // HALVES
+E_HALF = G_HALF * BAG
+LIST_HALF = E_HALF // 16
+M_HALF = M // HALVES
+TILES = M_HALF // P
+WIDTH = M_HALF + G_HALF
+
+
+def tile_attend_bag_bias_kernel(tc, xT, w, bias, offs, out):
+    nc = tc.nc
+    with ExitStack() as ctx:
+        keep = ctx.enter_context(tc.tile_pool(name="keep", bufs=1))
+        psum = ctx.enter_context(tc.psum_pool(name="psum", bufs=8))
+
+        offsets = keep.tile([P, G * BAG // 16], U16, name="offsets")
+        nc.sync.dma_start(offsets[:], offs)
+
+        x_rows = xT.rearrange("(p t) c -> p t c", t=PACK)
+        planes = []
+        for t in range(PACK):
+            plane = keep.tile([P, T], F32, name="plane%d" % t)
+            nc.sync.dma_start(plane[:], x_rows[:, t, :])
+            planes.append(plane)
+        w_rows = w.rearrange("(p t) m -> p t m", t=PACK)
+        w_raw = []
+        for h in range(HALVES):
+            raw = keep.tile([P, PACK, M_HALF], F32, name="w_raw%d" % h)
+            nc.sync.dma_start(raw[:], w_rows[:, :, h * M_HALF : (h + 1) * M_HALF])
+            w_raw.append(raw)
+        bias_cols = keep.tile([P, HALVES, TILES], F32, name="bias_cols")
+        nc.sync.dma_start(bias_cols[:], bias.rearrange("(h p u) o -> p h (u o)", h=HALVES, u=TILES))
+
+        zero = keep.tile([P, 1], F32, name="zero")
+        nc.vector.memset(zero[:], 0.0)
+        loaded = keep.tile([P, 1], F32, name="loaded")
+        nc.scalar.activation(loaded[:], zero[:], IDENTITY)
+
+        picked = [keep.tile([P, PACK, E_HALF], F32, name="picked%d" % h) for h in range(HALVES)]
+        grouped = [keep.tile([P, WIDTH, PACK], BF16, name="grouped%d" % h, align_bytes=64) for h in range(HALVES)]
+        codes = [keep.tile([P, WIDTH], U32, name="codes%d" % h, align_bytes=64) for h in range(HALVES)]
+        scales = [keep.tile([P, WIDTH], U8, name="scales%d" % h, align_bytes=64) for h in range(HALVES)]
+        def gather(t, h):
+            nc.vector.tensor_copy(
+                picked[h][:, t, :],
+                planes[t][:].indirect(offsets[:, h * LIST_HALF : (h + 1) * LIST_HALF]),
+            )
+
+        def add(t0, t1):
+            sums = [tile[:, M_HALF:, t0:t1] for tile in grouped]
+            pairs = picked[0][:].rearrange("p t (g j) -> p j g t", j=BAG)
+            nc.gpsimd.tensor_tensor(out=sums[0], in0=pairs[:, 0, :, t0:t1], in1=pairs[:, 1, :, t0:t1], op=ADD)
+            entries = picked[1][:].rearrange("p t (g j) -> p g t j", j=BAG)
+            with nc.allow_low_precision(reason="two float32 values are summed in float32; only the sum is rounded"):
+                nc.vector.tensor_reduce(out=sums[1], in_=entries[:, :, t0:t1, :], axis=mybir.AxisListType.X, op=ADD)
+
+        for t in range(PACK):
+            for h in range(HALVES):
+                gather(t, h)
+            if t > 0:
+                add(0 if t == 1 else t, t + 1)
+
+        for h in range(HALVES):
+            for u in range(TILES):
+                nc.scalar.activation(
+                    grouped[h][:, u * P : (u + 1) * P, :].rearrange("p (c i) t -> p c t i", i=4),
+                    w_raw[h][:].rearrange("p t (c i u) -> p u c t i", i=4, u=TILES)[:, u],
+                    IDENTITY,
+                )
+        for h in range(HALVES):
+            nc.vector.quantize_mx(
+                out=codes[h][:].bitcast(FP8X4), scales=scales[h][:], in_=grouped[h][:].rearrange("p c t -> p (c t)")
+            )
+
+        result = keep.tile([P, HALVES, TILES, G], F32, name="result")
+        out_rows = out.rearrange("(h p u) g -> p h u g", h=HALVES, u=TILES)
+
+        def multiply(wh, u, h):
+            half = slice(h * G_HALF, (h + 1) * G_HALF)
+            cols = slice(u * P, (u + 1) * P)
+            acc = psum.tile([P, 512], F32, name="acc")
+            nc.tensor.matmul_mx(
+                out=acc[:, 0:G_HALF],
+                lhsT=codes[wh][:, cols].bitcast(FP8X4),
+                lhsT_scale=scales[wh][:, cols],
+                rhs=codes[h][:, M_HALF:].bitcast(FP8X4),
+                rhs_scale=scales[h][:, M_HALF:],
+                start=True,
+                stop=True,
+            )
+            dst = result[:, wh, u, half]
+            b = bias_cols[:, wh, u : u + 1]
+            if h == 1:
+                nc.vector.tensor_scalar(dst, acc[:, 0:G_HALF], b, None, ADD)
+            else:
+                nc.scalar.activation(dst, acc[:, 0:G_HALF], IDENTITY, bias=b)
+
+        for h in range(HALVES):
+            half = slice(h * G_HALF, (h + 1) * G_HALF)
+            for u in range(TILES):
+                multiply(0, u, h)
+            nc.sync.dma_start(out_rows[:, 0, :, half], result[:, 0, :, half])
+        for u in range(TILES):
+            for h in range(HALVES):
+                multiply(1, u, h)
+            nc.sync.dma_start(out_rows[:, 1, u, :], result[:, 1, u, :])

@@ -1,6 +1,7 @@
 from contextlib import ExitStack
 
 import concourse.mybir as mybir
+from concourse.masks import make_identity
 
 D, T, G, BAG, M = 512, 4096, 512, 2, 512
 FLOPS = 2 * D * M * G
@@ -16,19 +17,16 @@ IDENTITY = mybir.ActivationFunctionType.Identity
 
 P = 128
 PACK = 4
-HALVES = 2
-G_HALF = G // HALVES
-E_HALF = G_HALF * BAG
-LIST_HALF = E_HALF // 16
-M_HALF = M // HALVES
-TILES = M_HALF // P
-WIDTH = M_HALF + G_HALF
+STAGES = 4
+ENTRIES = P * BAG
+LIST_COLS = ENTRIES // 16
 
 
 def tile_attend_bag_bias_kernel(tc, xT, w, bias, offs, out):
     nc = tc.nc
     with ExitStack() as ctx:
         keep = ctx.enter_context(tc.tile_pool(name="keep", bufs=1))
+        ring = ctx.enter_context(tc.tile_pool(name="ring", bufs=2))
         psum = ctx.enter_context(tc.psum_pool(name="psum", bufs=8))
 
         offsets = keep.tile([P, G * BAG // 16], U16, name="offsets")
@@ -42,83 +40,136 @@ def tile_attend_bag_bias_kernel(tc, xT, w, bias, offs, out):
             planes.append(plane)
         w_rows = w.rearrange("(p t) m -> p t m", t=PACK)
         w_raw = []
-        for h in range(HALVES):
-            raw = keep.tile([P, PACK, M_HALF], F32, name="w_raw%d" % h)
-            nc.sync.dma_start(raw[:], w_rows[:, :, h * M_HALF : (h + 1) * M_HALF])
+        for u in range(STAGES):
+            raw = keep.tile([P, PACK, P], F32, name="w_raw%d" % u, align_bytes=64)
+            nc.sync.dma_start(raw[:], w_rows[:, :, u * P : (u + 1) * P])
             w_raw.append(raw)
-        bias_cols = keep.tile([P, HALVES, TILES], F32, name="bias_cols")
-        nc.sync.dma_start(bias_cols[:], bias.rearrange("(h p u) o -> p h (u o)", h=HALVES, u=TILES))
 
-        zero = keep.tile([P, 1], F32, name="zero")
-        nc.vector.memset(zero[:], 0.0)
-        loaded = keep.tile([P, 1], F32, name="loaded")
-        nc.scalar.activation(loaded[:], zero[:], IDENTITY)
+        bias_rows = keep.tile([P, P], F32, name="bias_rows")
+        nc.vector.memset(bias_rows[:], 0.0)
+        nc.scalar.dma_start(bias_rows[0:STAGES, :], bias.rearrange("(u p) o -> u (p o)", p=P))
+        ident = keep.tile([P, P], F32, name="ident")
+        make_identity(nc, ident[:])
+        turned = psum.tile([P, 512], F32, name="acc")
+        nc.tensor.transpose(turned[:, 0:P], bias_rows[:], ident[:])
+        bias_cols = keep.tile([P, STAGES], F32, name="bias_cols")
+        nc.scalar.activation(bias_cols[:], turned[:, 0:STAGES], IDENTITY)
 
-        picked = [keep.tile([P, PACK, E_HALF], F32, name="picked%d" % h) for h in range(HALVES)]
-        grouped = [keep.tile([P, WIDTH, PACK], BF16, name="grouped%d" % h, align_bytes=64) for h in range(HALVES)]
-        codes = [keep.tile([P, WIDTH], U32, name="codes%d" % h, align_bytes=64) for h in range(HALVES)]
-        scales = [keep.tile([P, WIDTH], U8, name="scales%d" % h, align_bytes=64) for h in range(HALVES)]
-        def gather(t, h):
-            nc.vector.tensor_copy(
-                picked[h][:, t, :],
-                planes[t][:].indirect(offsets[:, h * LIST_HALF : (h + 1) * LIST_HALF]),
-            )
+        LAST = STAGES - 1
+        grouped = [keep.tile([P, 2 * P, PACK], BF16, name="grouped%d" % s, align_bytes=64) for s in range(LAST)]
+        w_in = [tile[:, 0:P, :] for tile in grouped] + [keep.tile([P, P, PACK], BF16, name="w_last", align_bytes=64)[:]]
+        e_in = [tile[:, P:, :] for tile in grouped] + [keep.tile([P, P, PACK], BF16, name="e_last", align_bytes=64)[:]]
 
-        def add(t0, t1):
-            sums = [tile[:, M_HALF:, t0:t1] for tile in grouped]
-            pairs = picked[0][:].rearrange("p t (g j) -> p j g t", j=BAG)
-            nc.gpsimd.tensor_tensor(out=sums[0], in0=pairs[:, 0, :, t0:t1], in1=pairs[:, 1, :, t0:t1], op=ADD)
-            entries = picked[1][:].rearrange("p t (g j) -> p g t j", j=BAG)
-            with nc.allow_low_precision(reason="two float32 values are summed in float32; only the sum is rounded"):
-                nc.vector.tensor_reduce(out=sums[1], in_=entries[:, :, t0:t1, :], axis=mybir.AxisListType.X, op=ADD)
+        def add(t, c, entries):
+            pairs = entries.rearrange("p (g j) -> p j g", j=BAG)
+            nc.gpsimd.tensor_tensor(out=e_in[c][:, :, t], in0=pairs[:, 0, :], in1=pairs[:, 1, :], op=ADD)
 
-        for t in range(PACK):
-            for h in range(HALVES):
-                gather(t, h)
-            if t > 0:
-                add(0 if t == 1 else t, t + 1)
-
-        for h in range(HALVES):
-            for u in range(TILES):
-                nc.scalar.activation(
-                    grouped[h][:, u * P : (u + 1) * P, :].rearrange("p (c i) t -> p c t i", i=4),
-                    w_raw[h][:].rearrange("p t (c i u) -> p u c t i", i=4, u=TILES)[:, u],
-                    IDENTITY,
+        for t in range(PACK - 1):
+            for h in range(2):
+                picked = ring.tile([P, 2 * ENTRIES], BF16, name="picked", bufs=4)
+                nc.vector.tensor_copy(
+                    picked[:], planes[t][:].indirect(offsets[:, 2 * h * LIST_COLS : 2 * (h + 1) * LIST_COLS])
                 )
-        for h in range(HALVES):
-            nc.vector.quantize_mx(
-                out=codes[h][:].bitcast(FP8X4), scales=scales[h][:], in_=grouped[h][:].rearrange("p c t -> p (c t)")
+                for c in range(2):
+                    add(t, 2 * h + c, picked[:, c * ENTRIES : (c + 1) * ENTRIES])
+
+        def gather_last(c, tag):
+            piece = keep.tile([P, ENTRIES], BF16, name="piece%d" % c, tag=tag, align_bytes=64)
+            nc.vector.tensor_copy(
+                piece[:], planes[PACK - 1][:].indirect(offsets[:, c * LIST_COLS : (c + 1) * LIST_COLS])
+            )
+            add(PACK - 1, c, piece[:])
+
+        def interleave(u):
+            nc.scalar.activation(
+                w_in[u].rearrange("p (c i) t -> p c t i", i=4),
+                w_raw[u][:].rearrange("p t (c i) -> p c t i", i=4),
+                IDENTITY,
             )
 
-        result = keep.tile([P, HALVES, TILES, G], F32, name="result")
-        out_rows = out.rearrange("(h p u) g -> p h u g", h=HALVES, u=TILES)
+        def quantize(values, name, tag):
+            width = values.shape[1]
+            codes = keep.tile([P, width], U32, name="codes" + name, tag=tag, align_bytes=64)
+            scales = keep.tile([P, width], U8, name="scales" + name, align_bytes=64)
+            nc.vector.quantize_mx(
+                out=codes[:].bitcast(FP8X4), scales=scales[:], in_=values.rearrange("p c t -> p (c t)")
+            )
+            return codes, scales
 
-        def multiply(wh, u, h):
-            half = slice(h * G_HALF, (h + 1) * G_HALF)
-            cols = slice(u * P, (u + 1) * P)
-            acc = psum.tile([P, 512], F32, name="acc")
+        w_mx, e_mx = [], []
+
+        def quantize_pair(s):
+            codes, scales = quantize(grouped[s][:], "%d" % s, "codes%d" % s)
+            w_mx.append((codes[:, 0:P], scales[:, 0:P]))
+            e_mx.append((codes[:, P:], scales[:, P:]))
+
+        for u in range(STAGES):
+            interleave(u)
+        for c in range(LAST):
+            gather_last(c, "piece%d" % c)
+        quantize_pair(0)
+        gather_last(LAST, "w_raw0")
+        quantize_pair(1)
+        quantize_pair(2)
+        codes, scales = quantize(w_in[LAST], "w", "codesw")
+        w_mx.append((codes[:], scales[:]))
+        codes, scales = quantize(e_in[LAST], "e", "grouped2")
+        e_mx.append((codes[:], scales[:]))
+
+        result = keep.tile([P, STAGES, G], F32, name="result")
+        out_rows = out.rearrange("(u p) g -> p u g", p=P)
+
+        def multiply(dst, u, c):
             nc.tensor.matmul_mx(
-                out=acc[:, 0:G_HALF],
-                lhsT=codes[wh][:, cols].bitcast(FP8X4),
-                lhsT_scale=scales[wh][:, cols],
-                rhs=codes[h][:, M_HALF:].bitcast(FP8X4),
-                rhs_scale=scales[h][:, M_HALF:],
+                out=dst,
+                lhsT=w_mx[u][0].bitcast(FP8X4),
+                lhsT_scale=w_mx[u][1],
+                rhs=e_mx[c][0].bitcast(FP8X4),
+                rhs_scale=e_mx[c][1],
                 start=True,
                 stop=True,
             )
-            dst = result[:, wh, u, half]
-            b = bias_cols[:, wh, u : u + 1]
-            if h == 1:
-                nc.vector.tensor_scalar(dst, acc[:, 0:G_HALF], b, None, ADD)
-            else:
-                nc.scalar.activation(dst, acc[:, 0:G_HALF], IDENTITY, bias=b)
 
-        for h in range(HALVES):
-            half = slice(h * G_HALF, (h + 1) * G_HALF)
-            for u in range(TILES):
-                multiply(0, u, h)
-            nc.sync.dma_start(out_rows[:, 0, :, half], result[:, 0, :, half])
-        for u in range(TILES):
-            for h in range(HALVES):
-                multiply(1, u, h)
-            nc.sync.dma_start(out_rows[:, 1, u, :], result[:, 1, u, :])
+        def row_part(u, c1):
+            acc = psum.tile([P, 512], F32, name="acc")
+            for c in range(c1):
+                multiply(acc[:, c * P : (c + 1) * P], u, c)
+            nc.scalar.activation(result[:, u, 0 : c1 * P], acc[:, 0 : c1 * P], IDENTITY, bias=bias_cols[:, u : u + 1])
+
+        def column_part(u0, u1, c, on_vector):
+            acc = psum.tile([P, 512], F32, name="acc")
+            for u in range(u0, u1):
+                multiply(acc[:, (u - u0) * P : (u - u0 + 1) * P], u, c)
+            cols = slice(c * P, (c + 1) * P)
+            if on_vector:
+                nc.vector.tensor_tensor(
+                    out=result[:, u0:u1, cols],
+                    in0=acc[:, 0 : (u1 - u0) * P].rearrange("p (u g) -> p u g", g=P),
+                    in1=bias_cols[:, u0:u1].unsqueeze(2).to_broadcast([P, u1 - u0, P]),
+                    op=ADD,
+                )
+            else:
+                for u in range(u0, u1):
+                    nc.scalar.activation(
+                        result[:, u, cols],
+                        acc[:, (u - u0) * P : (u - u0 + 1) * P],
+                        IDENTITY,
+                        bias=bias_cols[:, u : u + 1],
+                    )
+
+        def store(u0, u1, c0, c1):
+            nc.sync.dma_start(out_rows[:, u0:u1, c0 * P : c1 * P], result[:, u0:u1, c0 * P : c1 * P])
+
+        row_part(0, 2)
+        row_part(1, 2)
+        store(0, 2, 0, 2)
+        row_part(2, 3)
+        store(2, 3, 0, 3)
+        column_part(0, 2, 2, False)
+        store(0, 2, 2, 3)
+        row_part(3, 3)
+        store(3, 4, 0, 3)
+        column_part(0, 2, 3, True)
+        store(0, 2, 3, 4)
+        column_part(2, 4, 3, True)
+        store(2, 4, 3, 4)

@@ -30,7 +30,6 @@ def tile_attend_bag_bias_kernel(tc, xT, w, bias, offs, out):
         psum = ctx.enter_context(tc.psum_pool(name="psum", bufs=8))
 
         offsets = keep.tile([P, G * BAG // 16], U16, name="offsets")
-        nc.sync.dma_start(offsets[:], offs)
 
         x_rows = xT.rearrange("(p t) c -> p t c", t=PACK)
         planes = []
@@ -38,12 +37,14 @@ def tile_attend_bag_bias_kernel(tc, xT, w, bias, offs, out):
             plane = keep.tile([P, T], F32, name="plane%d" % t)
             nc.sync.dma_start(plane[:], x_rows[:, t, :])
             planes.append(plane)
+            if t == 0:
+                nc.sync.dma_start(offsets[:], offs)
         w_rows = w.rearrange("(p t) m -> p t m", t=PACK)
         w_raw = []
-        for u in range(STAGES):
-            raw = keep.tile([P, PACK, P], F32, name="w_raw%d" % u, align_bytes=64)
-            nc.sync.dma_start(raw[:], w_rows[:, :, u * P : (u + 1) * P])
-            w_raw.append(raw)
+        for u0, u1 in ((0, 2), (2, 3), (3, 4)):
+            raw = keep.tile([P, PACK, (u1 - u0) * P], F32, name="w_raw%d" % u0, align_bytes=64)
+            nc.sync.dma_start(raw[:], w_rows[:, :, u0 * P : u1 * P])
+            w_raw.extend(raw[:, :, i * P : (i + 1) * P] for i in range(u1 - u0))
 
         bias_rows = keep.tile([P, P], F32, name="bias_rows")
         nc.vector.memset(bias_rows[:], 0.0)
@@ -55,35 +56,40 @@ def tile_attend_bag_bias_kernel(tc, xT, w, bias, offs, out):
         bias_cols = keep.tile([P, STAGES], F32, name="bias_cols")
         nc.scalar.activation(bias_cols[:], turned[:, 0:STAGES], IDENTITY)
 
-        LAST = STAGES - 1
-        grouped = [keep.tile([P, 2 * P, PACK], BF16, name="grouped%d" % s, align_bytes=64) for s in range(LAST)]
-        w_in = [tile[:, 0:P, :] for tile in grouped] + [keep.tile([P, P, PACK], BF16, name="w_last", align_bytes=64)[:]]
-        e_in = [tile[:, P:, :] for tile in grouped] + [keep.tile([P, P, PACK], BF16, name="e_last", align_bytes=64)[:]]
+        grouped = [keep.tile([P, 2 * P, PACK], BF16, name="grouped%d" % s, align_bytes=64) for s in range(2)]
+        w_in = [tile[:, 0:P, :] for tile in grouped]
+        e_in = [tile[:, P:, :] for tile in grouped]
+        for s in range(2, STAGES):
+            w_in.append(keep.tile([P, P, PACK], BF16, name="w_in%d" % s, align_bytes=64)[:])
+            e_in.append(keep.tile([P, P, PACK], BF16, name="e_in%d" % s, align_bytes=64)[:])
 
-        def add(t, c, entries):
+        def gather(dst, t, c0, c1):
+            nc.vector.tensor_copy(dst, planes[t][:].indirect(offsets[:, c0 * LIST_COLS : c1 * LIST_COLS]))
+
+        def add(engine, dst, entries):
             pairs = entries.rearrange("p (g j) -> p j g", j=BAG)
-            nc.gpsimd.tensor_tensor(out=e_in[c][:, :, t], in0=pairs[:, 0, :], in1=pairs[:, 1, :], op=ADD)
+            engine.tensor_tensor(out=dst, in0=pairs[:, 0, :], in1=pairs[:, 1, :], op=ADD)
 
         for t in range(PACK - 1):
-            for h in range(2):
-                picked = ring.tile([P, 2 * ENTRIES], BF16, name="picked", bufs=4)
-                nc.vector.tensor_copy(
-                    picked[:], planes[t][:].indirect(offsets[:, 2 * h * LIST_COLS : 2 * (h + 1) * LIST_COLS])
-                )
-                for c in range(2):
-                    add(t, 2 * h + c, picked[:, c * ENTRIES : (c + 1) * ENTRIES])
+            first = ring.tile([P, 2 * ENTRIES], BF16, name="first")
+            gather(first[:], t, 0, 2)
+            second = ring.tile([P, 2 * ENTRIES], BF16, name="second")
+            gather(second[:], t, 2, 4)
+            for c in range(2):
+                add(nc.gpsimd, e_in[c][:, :, t], first[:, c * ENTRIES : (c + 1) * ENTRIES])
+                add(nc.vector, e_in[2 + c][:, :, t], second[:, c * ENTRIES : (c + 1) * ENTRIES])
 
-        def gather_last(c, tag):
-            piece = keep.tile([P, ENTRIES], BF16, name="piece%d" % c, tag=tag, align_bytes=64)
-            nc.vector.tensor_copy(
-                piece[:], planes[PACK - 1][:].indirect(offsets[:, c * LIST_COLS : (c + 1) * LIST_COLS])
-            )
-            add(PACK - 1, c, piece[:])
+        for c in range(2):
+            late = keep.tile([P, ENTRIES], BF16, name="late%d" % c)
+            gather(late[:], PACK - 1, c, c + 1)
+            add(nc.gpsimd, e_in[c][:, :, PACK - 1], late[:])
+        late_second = keep.tile([P, 2 * ENTRIES], BF16, name="late_second")
+        gather(late_second[:], PACK - 1, 2, 4)
 
         def interleave(u):
             nc.scalar.activation(
                 w_in[u].rearrange("p (c i) t -> p c t i", i=4),
-                w_raw[u][:].rearrange("p t (c i) -> p c t i", i=4),
+                w_raw[u].rearrange("p t (c i) -> p c t i", i=4),
                 IDENTITY,
             )
 
@@ -96,36 +102,35 @@ def tile_attend_bag_bias_kernel(tc, xT, w, bias, offs, out):
             )
             return codes, scales
 
+        for u in range(STAGES):
+            interleave(u)
         w_mx, e_mx = [], []
-
-        def quantize_pair(s):
+        for s in range(2):
             codes, scales = quantize(grouped[s][:], "%d" % s, "codes%d" % s)
             w_mx.append((codes[:, 0:P], scales[:, 0:P]))
             e_mx.append((codes[:, P:], scales[:, P:]))
-
-        for u in range(STAGES):
-            interleave(u)
-        for c in range(LAST):
-            gather_last(c, "piece%d" % c)
-        quantize_pair(0)
-        gather_last(LAST, "w_raw0")
-        quantize_pair(1)
-        quantize_pair(2)
-        codes, scales = quantize(w_in[LAST], "w", "codesw")
+        codes, scales = quantize(w_in[2], "w2", "codesw2")
         w_mx.append((codes[:], scales[:]))
-        codes, scales = quantize(e_in[LAST], "e", "grouped2")
-        e_mx.append((codes[:], scales[:]))
+        sums = keep.tile([P, 2 * P], BF16, name="sums", tag="w_raw2", align_bytes=64)
+        add(nc.vector, sums[:], late_second[:])
+        codes, scales = quantize(w_in[3], "w3", "codesw3")
+        w_mx.append((codes[:], scales[:]))
+        for s in range(2, STAGES):
+            nc.vector.tensor_copy(e_in[s][:, :, PACK - 1], sums[:, (s - 2) * P : (s - 1) * P])
+        for s in range(2, STAGES):
+            codes, scales = quantize(e_in[s], "e%d" % s, "codese%d" % s)
+            e_mx.append((codes[:], scales[:]))
 
         result = keep.tile([P, STAGES, G], F32, name="result")
         out_rows = out.rearrange("(u p) g -> p u g", p=P)
 
-        def multiply(dst, u, c):
+        def multiply(dst, u, moving):
             nc.tensor.matmul_mx(
                 out=dst,
                 lhsT=w_mx[u][0].bitcast(FP8X4),
                 lhsT_scale=w_mx[u][1],
-                rhs=e_mx[c][0].bitcast(FP8X4),
-                rhs_scale=e_mx[c][1],
+                rhs=moving[0].bitcast(FP8X4),
+                rhs_scale=moving[1],
                 start=True,
                 stop=True,
             )
@@ -133,13 +138,13 @@ def tile_attend_bag_bias_kernel(tc, xT, w, bias, offs, out):
         def row_part(u, c1):
             acc = psum.tile([P, 512], F32, name="acc")
             for c in range(c1):
-                multiply(acc[:, c * P : (c + 1) * P], u, c)
+                multiply(acc[:, c * P : (c + 1) * P], u, e_mx[c])
             nc.scalar.activation(result[:, u, 0 : c1 * P], acc[:, 0 : c1 * P], IDENTITY, bias=bias_cols[:, u : u + 1])
 
         def column_part(u0, u1, c, on_vector):
             acc = psum.tile([P, 512], F32, name="acc")
             for u in range(u0, u1):
-                multiply(acc[:, (u - u0) * P : (u - u0 + 1) * P], u, c)
+                multiply(acc[:, (u - u0) * P : (u - u0 + 1) * P], u, e_mx[c])
             cols = slice(c * P, (c + 1) * P)
             if on_vector:
                 nc.vector.tensor_tensor(
@@ -160,16 +165,15 @@ def tile_attend_bag_bias_kernel(tc, xT, w, bias, offs, out):
         def store(u0, u1, c0, c1):
             nc.sync.dma_start(out_rows[:, u0:u1, c0 * P : c1 * P], result[:, u0:u1, c0 * P : c1 * P])
 
-        row_part(0, 2)
-        row_part(1, 2)
-        store(0, 2, 0, 2)
-        row_part(2, 3)
-        store(2, 3, 0, 3)
-        column_part(0, 2, 2, False)
+        for u in range(STAGES):
+            row_part(u, 2)
+            store(u, u + 1, 0, 2)
+        column_part(0, 2, 2, True)
         store(0, 2, 2, 3)
-        row_part(3, 3)
-        store(3, 4, 0, 3)
-        column_part(0, 2, 3, True)
+        column_part(2, 4, 2, True)
+        store(2, 4, 2, 3)
+        column_part(0, 2, 3, False)
         store(0, 2, 3, 4)
-        column_part(2, 4, 3, True)
+        column_part(2, 3, 3, True)
+        column_part(3, 4, 3, False)
         store(2, 4, 3, 4)

@@ -19,7 +19,7 @@ P = 128
 PACK = 4
 STAGES = 4
 ENTRIES = P * BAG
-LIST_COLS = ENTRIES // 16
+SPLIT = 320
 
 
 def tile_attend_bag_bias_kernel(tc, xT, w, bias, offs, out):
@@ -56,35 +56,29 @@ def tile_attend_bag_bias_kernel(tc, xT, w, bias, offs, out):
         bias_cols = keep.tile([P, STAGES], F32, name="bias_cols")
         nc.scalar.activation(bias_cols[:], turned[:, 0:STAGES], IDENTITY)
 
-        grouped = [keep.tile([P, 2 * P, PACK], BF16, name="grouped%d" % s, align_bytes=64) for s in range(2)]
-        w_in = [tile[:, 0:P, :] for tile in grouped]
-        e_in = [tile[:, P:, :] for tile in grouped]
-        for s in range(2, STAGES):
+        front = keep.tile([P, P + G, PACK], BF16, name="front", align_bytes=64)
+        bags = front[:, P:, :]
+        w_in = [front[:, 0:P, :]]
+        for s in range(1, STAGES):
             w_in.append(keep.tile([P, P, PACK], BF16, name="w_in%d" % s, align_bytes=64)[:])
-            e_in.append(keep.tile([P, P, PACK], BF16, name="e_in%d" % s, align_bytes=64)[:])
+        e_in = [bags[:, c * P : (c + 1) * P, :] for c in range(STAGES)]
 
-        def gather(dst, t, c0, c1):
-            nc.vector.tensor_copy(dst, planes[t][:].indirect(offsets[:, c0 * LIST_COLS : c1 * LIST_COLS]))
+        def gather(name, t, g0, g1, pool):
+            picked = pool.tile([P, (g1 - g0) * BAG], BF16, name=name)
+            nc.vector.tensor_copy(picked[:], planes[t][:].indirect(offsets[:, g0 * BAG // 16 : g1 * BAG // 16]))
+            return picked[:]
 
         def add(engine, dst, entries):
             pairs = entries.rearrange("p (g j) -> p j g", j=BAG)
             engine.tensor_tensor(out=dst, in0=pairs[:, 0, :], in1=pairs[:, 1, :], op=ADD)
 
         for t in range(PACK - 1):
-            first = ring.tile([P, 2 * ENTRIES], BF16, name="first")
-            gather(first[:], t, 0, 2)
-            second = ring.tile([P, 2 * ENTRIES], BF16, name="second")
-            gather(second[:], t, 2, 4)
-            for c in range(2):
-                add(nc.gpsimd, e_in[c][:, :, t], first[:, c * ENTRIES : (c + 1) * ENTRIES])
-                add(nc.vector, e_in[2 + c][:, :, t], second[:, c * ENTRIES : (c + 1) * ENTRIES])
+            add(nc.gpsimd, bags[:, 0:SPLIT, t], gather("first", t, 0, SPLIT, ring))
+            add(nc.vector, bags[:, SPLIT:, t], gather("second", t, SPLIT, G, ring))
 
-        for c in range(2):
-            late = keep.tile([P, ENTRIES], BF16, name="late%d" % c)
-            gather(late[:], PACK - 1, c, c + 1)
-            add(nc.gpsimd, e_in[c][:, :, PACK - 1], late[:])
-        late_second = keep.tile([P, 2 * ENTRIES], BF16, name="late_second")
-        gather(late_second[:], PACK - 1, 2, 4)
+        for g0, g1 in ((0, 64), (64, 192), (192, SPLIT)):
+            add(nc.gpsimd, bags[:, g0:g1, PACK - 1], gather("late%d" % g0, PACK - 1, g0, g1, keep))
+        late_second = gather("late_second", PACK - 1, SPLIT, G, keep)
 
         def interleave(u):
             nc.scalar.activation(
@@ -104,22 +98,31 @@ def tile_attend_bag_bias_kernel(tc, xT, w, bias, offs, out):
 
         for u in range(STAGES):
             interleave(u)
-        w_mx, e_mx = [], []
-        for s in range(2):
-            codes, scales = quantize(grouped[s][:], "%d" % s, "codes%d" % s)
-            w_mx.append((codes[:, 0:P], scales[:, 0:P]))
-            e_mx.append((codes[:, P:], scales[:, P:]))
+        codes, scales = quantize(front[:, 0 : 2 * P, :], "0", "codes0")
+        w_mx = [(codes[:, 0:P], scales[:, 0:P])]
+        e_mx = [(codes[:, P:], scales[:, P:])]
+        codes, scales = quantize(e_in[1], "e1", "w_raw0")
+        e_mx.append((codes[:], scales[:]))
+        codes, scales = quantize(w_in[1], "w1", "codesw1")
+        w_mx.append((codes[:], scales[:]))
         codes, scales = quantize(w_in[2], "w2", "codesw2")
         w_mx.append((codes[:], scales[:]))
-        sums = keep.tile([P, 2 * P], BF16, name="sums", tag="w_raw2", align_bytes=64)
-        add(nc.vector, sums[:], late_second[:])
+        sums = keep.tile([P, G - SPLIT], BF16, name="sums", tag="w_raw2", align_bytes=64)
+        add(nc.vector, sums[:], late_second)
         codes, scales = quantize(w_in[3], "w3", "codesw3")
         w_mx.append((codes[:], scales[:]))
+        for g0, g1 in ((SPLIT, 3 * P), (3 * P, G)):
+            nc.vector.tensor_copy(bags[:, g0:g1, PACK - 1], sums[:, g0 - SPLIT : g1 - SPLIT])
+        late_codes = keep.tile([P, 2 * P], U32, name="late_codes", align_bytes=64)
+        late_scales = keep.tile([P, 2 * P], U8, name="late_scales", align_bytes=64)
         for s in range(2, STAGES):
-            nc.vector.tensor_copy(e_in[s][:, :, PACK - 1], sums[:, (s - 2) * P : (s - 1) * P])
-        for s in range(2, STAGES):
-            codes, scales = quantize(e_in[s], "e%d" % s, "codese%d" % s)
-            e_mx.append((codes[:], scales[:]))
+            cols = slice((s - 2) * P, (s - 1) * P)
+            nc.vector.quantize_mx(
+                out=late_codes[:, cols].bitcast(FP8X4),
+                scales=late_scales[:, cols],
+                in_=e_in[s].rearrange("p c t -> p (c t)"),
+            )
+            e_mx.append((late_codes[:, cols], late_scales[:, cols]))
 
         result = keep.tile([P, STAGES, G], F32, name="result")
         out_rows = out.rearrange("(u p) g -> p u g", p=P)
@@ -141,26 +144,12 @@ def tile_attend_bag_bias_kernel(tc, xT, w, bias, offs, out):
                 multiply(acc[:, c * P : (c + 1) * P], u, e_mx[c])
             nc.scalar.activation(result[:, u, 0 : c1 * P], acc[:, 0 : c1 * P], IDENTITY, bias=bias_cols[:, u : u + 1])
 
-        def column_part(u0, u1, c, on_vector):
-            acc = psum.tile([P, 512], F32, name="acc")
-            for u in range(u0, u1):
-                multiply(acc[:, (u - u0) * P : (u - u0 + 1) * P], u, e_mx[c])
-            cols = slice(c * P, (c + 1) * P)
+        def empty(acc, u, c0, c1, on_vector):
+            dst, src, b = result[:, u, c0 * P : c1 * P], acc[:, 0 : (c1 - c0) * P], bias_cols[:, u : u + 1]
             if on_vector:
-                nc.vector.tensor_tensor(
-                    out=result[:, u0:u1, cols],
-                    in0=acc[:, 0 : (u1 - u0) * P].rearrange("p (u g) -> p u g", g=P),
-                    in1=bias_cols[:, u0:u1].unsqueeze(2).to_broadcast([P, u1 - u0, P]),
-                    op=ADD,
-                )
+                nc.vector.tensor_scalar(dst, src, b, None, ADD)
             else:
-                for u in range(u0, u1):
-                    nc.scalar.activation(
-                        result[:, u, cols],
-                        acc[:, (u - u0) * P : (u - u0 + 1) * P],
-                        IDENTITY,
-                        bias=bias_cols[:, u : u + 1],
-                    )
+                nc.scalar.activation(dst, src, IDENTITY, bias=b)
 
         def store(u0, u1, c0, c1):
             nc.sync.dma_start(out_rows[:, u0:u1, c0 * P : c1 * P], result[:, u0:u1, c0 * P : c1 * P])
@@ -168,12 +157,19 @@ def tile_attend_bag_bias_kernel(tc, xT, w, bias, offs, out):
         for u in range(STAGES):
             row_part(u, 2)
             store(u, u + 1, 0, 2)
-        column_part(0, 2, 2, True)
-        store(0, 2, 2, 3)
-        column_part(2, 4, 2, True)
-        store(2, 4, 2, 3)
-        column_part(0, 2, 3, False)
-        store(0, 2, 3, 4)
-        column_part(2, 3, 3, True)
-        column_part(3, 4, 3, False)
-        store(2, 4, 3, 4)
+        banks = [psum.tile([P, 512], F32, name="acc") for u in range(2)]
+        for c in range(2, STAGES):
+            for u in range(2):
+                multiply(banks[u][:, (c - 2) * P : (c - 1) * P], u, e_mx[c])
+        for u in range(2):
+            empty(banks[u], u, 2, 4, u == 0)
+            store(u, u + 1, 2, 4)
+        acc = psum.tile([P, 512], F32, name="acc")
+        multiply(acc[:, 0 : 2 * P], 2, (late_codes[:], late_scales[:]))
+        empty(acc, 2, 2, 4, True)
+        store(2, 3, 2, 4)
+        for c in range(2, STAGES):
+            acc = psum.tile([P, 512], F32, name="acc")
+            multiply(acc[:, 0:P], 3, e_mx[c])
+            empty(acc, 3, c, c + 1, c == 3)
+        store(3, 4, 2, 4)

@@ -56,12 +56,19 @@ def tile_attend_bag_bias_kernel(tc, xT, w, bias, offs, out):
         bias_cols = keep.tile([P, STAGES], F32, name="bias_cols")
         nc.scalar.activation(bias_cols[:], turned[:, 0:STAGES], IDENTITY)
 
-        front = keep.tile([P, P + G, PACK], BF16, name="front", align_bytes=64)
-        bags = front[:, P:, :]
-        w_in = [front[:, 0:P, :]]
-        for s in range(1, STAGES):
+        grouped = [keep.tile([P, 2 * P, PACK], BF16, name="grouped%d" % s, align_bytes=64) for s in range(2)]
+        late_in = keep.tile([P, 2 * P, PACK], BF16, name="late_in", align_bytes=64)
+        w_in = [tile[:, 0:P, :] for tile in grouped]
+        for s in range(2, STAGES):
             w_in.append(keep.tile([P, P, PACK], BF16, name="w_in%d" % s, align_bytes=64)[:])
-        e_in = [bags[:, c * P : (c + 1) * P, :] for c in range(STAGES)]
+
+        def bags(g0, g1):
+            if g0 < 2 * P:
+                return grouped[g0 // P][:, P + g0 % P : P + g0 % P + g1 - g0, :]
+            return late_in[:, g0 - 2 * P : g1 - 2 * P, :]
+
+        e_in = [bags(c * P, (c + 1) * P) for c in range(STAGES)]
+        pool_runs = ((2 * P, SPLIT), (0, P), (P, 2 * P))
 
         def gather(name, t, g0, g1, pool):
             picked = pool.tile([P, (g1 - g0) * BAG], BF16, name=name)
@@ -73,11 +80,13 @@ def tile_attend_bag_bias_kernel(tc, xT, w, bias, offs, out):
             engine.tensor_tensor(out=dst, in0=pairs[:, 0, :], in1=pairs[:, 1, :], op=ADD)
 
         for t in range(PACK - 1):
-            add(nc.gpsimd, bags[:, 0:SPLIT, t], gather("first", t, 0, SPLIT, ring))
-            add(nc.vector, bags[:, SPLIT:, t], gather("second", t, SPLIT, G, ring))
+            first = gather("first", t, 0, SPLIT, ring)
+            for g0, g1 in pool_runs:
+                add(nc.gpsimd, bags(g0, g1)[:, :, t], first[:, g0 * BAG : g1 * BAG])
+            add(nc.vector, bags(SPLIT, G)[:, :, t], gather("second", t, SPLIT, G, ring))
 
-        for g0, g1 in ((0, 64), (64, 192), (192, SPLIT)):
-            add(nc.gpsimd, bags[:, g0:g1, PACK - 1], gather("late%d" % g0, PACK - 1, g0, g1, keep))
+        for g0, g1 in pool_runs:
+            add(nc.gpsimd, bags(g0, g1)[:, :, PACK - 1], gather("late%d" % g0, PACK - 1, g0, g1, keep))
         late_second = gather("late_second", PACK - 1, SPLIT, G, keep)
 
         def interleave(u):
@@ -98,22 +107,22 @@ def tile_attend_bag_bias_kernel(tc, xT, w, bias, offs, out):
 
         for u in range(STAGES):
             interleave(u)
-        codes, scales = quantize(front[:, 0 : 2 * P, :], "0", "codes0")
-        w_mx = [(codes[:, 0:P], scales[:, 0:P])]
-        e_mx = [(codes[:, P:], scales[:, P:])]
-        codes, scales = quantize(e_in[1], "e1", "w_raw0")
-        e_mx.append((codes[:], scales[:]))
-        codes, scales = quantize(w_in[1], "w1", "codesw1")
-        w_mx.append((codes[:], scales[:]))
+        w_mx, e_mx = [], []
+
+        def quantize_pair(s):
+            codes, scales = quantize(grouped[s][:], "%d" % s, "codes%d" % s)
+            w_mx.append((codes[:, 0:P], scales[:, 0:P]))
+            e_mx.append((codes[:, P:], scales[:, P:]))
+
+        quantize_pair(0)
+        sums = w_raw[0][:, 0, 0 : (G - SPLIT) // 2].bitcast(BF16)
+        add(nc.vector, sums, late_second)
+        quantize_pair(1)
+        for g0, g1 in ((SPLIT, 3 * P), (3 * P, G)):
+            nc.vector.tensor_copy(bags(g0, g1)[:, :, PACK - 1], sums[:, g0 - SPLIT : g1 - SPLIT])
         codes, scales = quantize(w_in[2], "w2", "codesw2")
         w_mx.append((codes[:], scales[:]))
-        sums = keep.tile([P, G - SPLIT], BF16, name="sums", tag="w_raw2", align_bytes=64)
-        add(nc.vector, sums[:], late_second)
-        codes, scales = quantize(w_in[3], "w3", "codesw3")
-        w_mx.append((codes[:], scales[:]))
-        for g0, g1 in ((SPLIT, 3 * P), (3 * P, G)):
-            nc.vector.tensor_copy(bags[:, g0:g1, PACK - 1], sums[:, g0 - SPLIT : g1 - SPLIT])
-        late_codes = keep.tile([P, 2 * P], U32, name="late_codes", align_bytes=64)
+        late_codes = keep.tile([P, 2 * P], U32, name="late_codes", tag="w_raw2", align_bytes=64)
         late_scales = keep.tile([P, 2 * P], U8, name="late_scales", align_bytes=64)
         for s in range(2, STAGES):
             cols = slice((s - 2) * P, (s - 1) * P)
@@ -123,6 +132,8 @@ def tile_attend_bag_bias_kernel(tc, xT, w, bias, offs, out):
                 in_=e_in[s].rearrange("p c t -> p (c t)"),
             )
             e_mx.append((late_codes[:, cols], late_scales[:, cols]))
+        codes, scales = quantize(w_in[3], "w3", "codesw3")
+        w_mx.append((codes[:], scales[:]))
 
         result = keep.tile([P, STAGES, G], F32, name="result")
         out_rows = out.rearrange("(u p) g -> p u g", p=P)
@@ -138,12 +149,6 @@ def tile_attend_bag_bias_kernel(tc, xT, w, bias, offs, out):
                 stop=True,
             )
 
-        def row_part(u, c1):
-            acc = psum.tile([P, 512], F32, name="acc")
-            for c in range(c1):
-                multiply(acc[:, c * P : (c + 1) * P], u, e_mx[c])
-            nc.scalar.activation(result[:, u, 0 : c1 * P], acc[:, 0 : c1 * P], IDENTITY, bias=bias_cols[:, u : u + 1])
-
         def empty(acc, u, c0, c1, on_vector):
             dst, src, b = result[:, u, c0 * P : c1 * P], acc[:, 0 : (c1 - c0) * P], bias_cols[:, u : u + 1]
             if on_vector:
@@ -154,22 +159,25 @@ def tile_attend_bag_bias_kernel(tc, xT, w, bias, offs, out):
         def store(u0, u1, c0, c1):
             nc.sync.dma_start(out_rows[:, u0:u1, c0 * P : c1 * P], result[:, u0:u1, c0 * P : c1 * P])
 
-        for u in range(STAGES):
-            row_part(u, 2)
-            store(u, u + 1, 0, 2)
-        banks = [psum.tile([P, 512], F32, name="acc") for u in range(2)]
-        for c in range(2, STAGES):
-            for u in range(2):
-                multiply(banks[u][:, (c - 2) * P : (c - 1) * P], u, e_mx[c])
-        for u in range(2):
-            empty(banks[u], u, 2, 4, u == 0)
-            store(u, u + 1, 2, 4)
-        acc = psum.tile([P, 512], F32, name="acc")
-        multiply(acc[:, 0 : 2 * P], 2, (late_codes[:], late_scales[:]))
-        empty(acc, 2, 2, 4, True)
-        store(2, 3, 2, 4)
-        for c in range(2, STAGES):
+        def part(u, c0, c1, on_vector):
             acc = psum.tile([P, 512], F32, name="acc")
-            multiply(acc[:, 0:P], 3, e_mx[c])
-            empty(acc, 3, c, c + 1, c == 3)
-        store(3, 4, 2, 4)
+            if (c0, c1) == (2, 4):
+                multiply(acc[:, 0 : 2 * P], u, (late_codes[:], late_scales[:]))
+            else:
+                for c in range(c0, c1):
+                    multiply(acc[:, (c - c0) * P : (c - c0 + 1) * P], u, e_mx[c])
+            empty(acc, u, c0, c1, on_vector)
+
+        part(0, 0, 1, False)
+        part(0, 1, 2, False)
+        store(0, 1, 0, 2)
+        for u in range(1, 3):
+            part(u, 0, 2, False)
+            store(u, u + 1, 0, 2)
+        for u in range(3):
+            part(u, 2, 4, u != 1)
+            store(u, u + 1, 2, 4)
+        part(3, 0, 2, False)
+        part(3, 2, 3, True)
+        part(3, 3, 4, True)
+        store(3, 4, 0, 4)

@@ -171,11 +171,16 @@ def tile_attend_bag_bias_kernel(tc, xT, w, bias, offs, out):
         part(0, 0, 1, False)
         part(0, 1, 2, False)
         store(0, 1, 0, 2)
+        part(1, 0, 2, False)
+        store(1, 2, 0, 2)
+        part(2, 0, 1, False)
+        part(2, 1, 2, False)
+        store(2, 3, 0, 2)
+        part(0, 2, 3, False)
+        part(0, 3, 4, True)
+        store(0, 1, 2, 4)
         for u in range(1, 3):
-            part(u, 0, 2, False)
-            store(u, u + 1, 0, 2)
-        for u in range(3):
-            part(u, 2, 4, u != 1)
+            part(u, 2, 4, u == 2)
             store(u, u + 1, 2, 4)
         part(3, 0, 2, False)
         part(3, 2, 3, True)

@@ -26,19 +26,19 @@ def tile_attend_bag_bias_kernel(tc, xT, w, bias, offs, out):
     nc = tc.nc
     with ExitStack() as ctx:
         keep = ctx.enter_context(tc.tile_pool(name="keep", bufs=1))
-        ring = ctx.enter_context(tc.tile_pool(name="ring", bufs=2))
         psum = ctx.enter_context(tc.psum_pool(name="psum", bufs=8))
 
         offsets = keep.tile([P, G * BAG // 16], U16, name="offsets")
 
         x_rows = xT.rearrange("(p t) c -> p t c", t=PACK)
-        planes = []
-        for t in range(PACK):
+        pair = keep.tile([P, 2 * T], F32, name="pair")
+        nc.sync.dma_start(pair[:], xT.rearrange("(p h t) c -> p h (t c)", h=2, t=2)[:, 0, :])
+        nc.sync.dma_start(offsets[:], offs)
+        planes = [pair[:, 0:T], pair[:, T:]]
+        for t in range(2, PACK):
             plane = keep.tile([P, T], F32, name="plane%d" % t)
             nc.sync.dma_start(plane[:], x_rows[:, t, :])
-            planes.append(plane)
-            if t == 0:
-                nc.sync.dma_start(offsets[:], offs)
+            planes.append(plane[:])
         w_rows = w.rearrange("(p t) m -> p t m", t=PACK)
         w_raw = []
         for u0, u1 in ((0, 2), (2, 3), (3, 4)):
@@ -72,18 +72,20 @@ def tile_attend_bag_bias_kernel(tc, xT, w, bias, offs, out):
 
         def gather(name, t, g0, g1, pool):
             picked = pool.tile([P, (g1 - g0) * BAG], BF16, name=name)
-            nc.vector.tensor_copy(picked[:], planes[t][:].indirect(offsets[:, g0 * BAG // 16 : g1 * BAG // 16]))
+            nc.vector.tensor_copy(picked[:], planes[t].indirect(offsets[:, g0 * BAG // 16 : g1 * BAG // 16]))
             return picked[:]
 
         def add(engine, dst, entries):
             pairs = entries.rearrange("p (g j) -> p j g", j=BAG)
             engine.tensor_tensor(out=dst, in0=pairs[:, 0, :], in1=pairs[:, 1, :], op=ADD)
 
+        early = keep.tile([P, PACK - 1, G * BAG], F32, name="early")
         for t in range(PACK - 1):
-            first = gather("first", t, 0, SPLIT, ring)
-            for g0, g1 in pool_runs:
-                add(nc.gpsimd, bags(g0, g1)[:, :, t], first[:, g0 * BAG : g1 * BAG])
-            add(nc.vector, bags(SPLIT, G)[:, :, t], gather("second", t, SPLIT, G, ring))
+            for runs in (((0, P), (P, 2 * P)), ((2 * P, G),)):
+                c0, c1 = runs[0][0] * BAG, runs[-1][1] * BAG
+                nc.vector.tensor_copy(early[:, t, c0:c1], planes[t].indirect(offsets[:, c0 // 16 : c1 // 16]))
+                for g0, g1 in runs:
+                    add(nc.gpsimd, bags(g0, g1)[:, :, t], early[:, t, g0 * BAG : g1 * BAG])
 
         for g0, g1 in pool_runs:
             add(nc.gpsimd, bags(g0, g1)[:, :, PACK - 1], gather("late%d" % g0, PACK - 1, g0, g1, keep))
@@ -183,6 +185,7 @@ def tile_attend_bag_bias_kernel(tc, xT, w, bias, offs, out):
             part(u, 2, 4, u == 2)
             store(u, u + 1, 2, 4)
         part(3, 0, 2, False)
+        store(3, 4, 0, 2)
         part(3, 2, 3, True)
         part(3, 3, 4, True)
-        store(3, 4, 0, 4)
+        store(3, 4, 2, 4)

@@ -56,15 +56,15 @@ def tile_attend_bag_bias_kernel(tc, xT, w, bias, offs, out):
         bias_cols = keep.tile([P, STAGES], F32, name="bias_cols")
         nc.scalar.activation(bias_cols[:], turned[:, 0:STAGES], IDENTITY)
 
-        grouped = [keep.tile([P, 2 * P, PACK], BF16, name="grouped%d" % s, align_bytes=64) for s in range(2)]
+        grouped = keep.tile([P, 4 * P, PACK], BF16, name="grouped", align_bytes=64)
         late_in = keep.tile([P, 2 * P, PACK], BF16, name="late_in", align_bytes=64)
-        w_in = [tile[:, 0:P, :] for tile in grouped]
+        w_in = [grouped[:, 0:P, :], grouped[:, 3 * P : 4 * P, :]]
         for s in range(2, STAGES):
             w_in.append(keep.tile([P, P, PACK], BF16, name="w_in%d" % s, align_bytes=64)[:])
 
         def bags(g0, g1):
             if g0 < 2 * P:
-                return grouped[g0 // P][:, P + g0 % P : P + g0 % P + g1 - g0, :]
+                return grouped[:, P + g0 : P + g1, :]
             return late_in[:, g0 - 2 * P : g1 - 2 * P, :]
 
         e_in = [bags(c * P, (c + 1) * P) for c in range(STAGES)]
@@ -111,20 +111,31 @@ def tile_attend_bag_bias_kernel(tc, xT, w, bias, offs, out):
             interleave(u)
         w_mx, e_mx = [], []
 
+        early_codes = keep.tile([P, 4 * P], U32, name="early_codes", align_bytes=64)
+        early_scales = keep.tile([P, 4 * P], U8, name="early_scales", align_bytes=64)
+        w_mx.extend((early_codes[:, c0 : c0 + P], early_scales[:, c0 : c0 + P]) for c0 in (0, 3 * P))
+        e_mx.extend((early_codes[:, c0 : c0 + P], early_scales[:, c0 : c0 + P]) for c0 in (P, 2 * P))
+        early = (early_codes[:, P : 3 * P], early_scales[:, P : 3 * P])
+
         def quantize_pair(s):
-            codes, scales = quantize(grouped[s][:], "%d" % s, "codes%d" % s)
-            w_mx.append((codes[:, 0:P], scales[:, 0:P]))
-            e_mx.append((codes[:, P:], scales[:, P:]))
+            cols = slice(2 * P * s, 2 * P * (s + 1))
+            nc.vector.quantize_mx(
+                out=early_codes[:, cols].bitcast(FP8X4),
+                scales=early_scales[:, cols],
+                in_=grouped[:, cols, :].rearrange("p c t -> p (c t)"),
+            )
 
         quantize_pair(0)
-        sums = w_raw[0][:, 0, 0 : (G - SPLIT) // 2].bitcast(BF16)
-        add(nc.vector, sums, late_second)
         quantize_pair(1)
-        for g0, g1 in ((SPLIT, 3 * P), (3 * P, G)):
-            nc.vector.tensor_copy(bags(g0, g1)[:, :, PACK - 1], sums[:, g0 - SPLIT : g1 - SPLIT])
+        sums = w_raw[2][:, 0, 0 : (G - SPLIT) // 2].bitcast(BF16)
+        add(nc.vector, sums, late_second)
         codes, scales = quantize(w_in[2], "w2", "codesw2")
         w_mx.append((codes[:], scales[:]))
-        late_codes = keep.tile([P, 2 * P], U32, name="late_codes", tag="w_raw2", align_bytes=64)
+        for g0, g1 in ((SPLIT, 3 * P), (3 * P, G)):
+            nc.vector.tensor_copy(bags(g0, g1)[:, :, PACK - 1], sums[:, g0 - SPLIT : g1 - SPLIT])
+        codes, scales = quantize(w_in[3], "w3", "codesw3")
+        w_mx.append((codes[:], scales[:]))
+        late_codes = keep.tile([P, 2 * P], U32, name="late_codes", tag="w_raw3", align_bytes=64)
         late_scales = keep.tile([P, 2 * P], U8, name="late_scales", align_bytes=64)
         for s in range(2, STAGES):
             cols = slice((s - 2) * P, (s - 1) * P)
@@ -134,8 +145,6 @@ def tile_attend_bag_bias_kernel(tc, xT, w, bias, offs, out):
                 in_=e_in[s].rearrange("p c t -> p (c t)"),
             )
             e_mx.append((late_codes[:, cols], late_scales[:, cols]))
-        codes, scales = quantize(w_in[3], "w3", "codesw3")
-        w_mx.append((codes[:], scales[:]))
 
         result = keep.tile([P, STAGES, G], F32, name="result")
         out_rows = out.rearrange("(u p) g -> p u g", p=P)
@@ -165,6 +174,8 @@ def tile_attend_bag_bias_kernel(tc, xT, w, bias, offs, out):
             acc = psum.tile([P, 512], F32, name="acc")
             if (c0, c1) == (2, 4):
                 multiply(acc[:, 0 : 2 * P], u, (late_codes[:], late_scales[:]))
+            elif (c0, c1) == (0, 2):
+                multiply(acc[:, 0 : 2 * P], u, early)
             else:
                 for c in range(c0, c1):
                     multiply(acc[:, (c - c0) * P : (c - c0 + 1) * P], u, e_mx[c])
@@ -173,19 +184,15 @@ def tile_attend_bag_bias_kernel(tc, xT, w, bias, offs, out):
         part(0, 0, 1, False)
         part(0, 1, 2, False)
         store(0, 1, 0, 2)
-        part(1, 0, 2, False)
-        store(1, 2, 0, 2)
-        part(2, 0, 1, False)
-        part(2, 1, 2, False)
-        store(2, 3, 0, 2)
+        for u in range(1, STAGES):
+            part(u, 0, 2, False)
+            store(u, u + 1, 0, 2)
         part(0, 2, 3, False)
         part(0, 3, 4, True)
         store(0, 1, 2, 4)
         for u in range(1, 3):
             part(u, 2, 4, u == 2)
             store(u, u + 1, 2, 4)
-        part(3, 0, 2, False)
-        store(3, 4, 0, 2)
-        part(3, 2, 3, True)
+        part(3, 2, 3, False)
         part(3, 3, 4, True)
         store(3, 4, 2, 4)

@@ -127,24 +127,26 @@ def tile_attend_bag_bias_kernel(tc, xT, w, bias, offs, out):
 
         quantize_pair(0)
         quantize_pair(1)
+        extra = quantize(bags(2 * P, SPLIT), "extra", "w_raw0")
         sums = w_raw[2][:, 0, 0 : (G - SPLIT) // 2].bitcast(BF16)
         add(nc.vector, sums, late_second)
         codes, scales = quantize(w_in[2], "w2", "codesw2")
         w_mx.append((codes[:], scales[:]))
-        for g0, g1 in ((SPLIT, 3 * P), (3 * P, G)):
+        for g0, g1 in ((SPLIT, SPLIT + P), (SPLIT + P, G)):
             nc.vector.tensor_copy(bags(g0, g1)[:, :, PACK - 1], sums[:, g0 - SPLIT : g1 - SPLIT])
         codes, scales = quantize(w_in[3], "w3", "codesw3")
         w_mx.append((codes[:], scales[:]))
-        late_codes = keep.tile([P, 2 * P], U32, name="late_codes", tag="w_raw3", align_bytes=64)
-        late_scales = keep.tile([P, 2 * P], U8, name="late_scales", align_bytes=64)
-        for s in range(2, STAGES):
-            cols = slice((s - 2) * P, (s - 1) * P)
+        late_codes = keep.tile([P, G - SPLIT], U32, name="late_codes", tag="w_raw3", align_bytes=64)
+        late_scales = keep.tile([P, G - SPLIT], U8, name="late_scales", align_bytes=64)
+        moving = {(0, P): e_mx[0], (P, 2 * P): e_mx[1], (0, 2 * P): early, (2 * P, SPLIT): (extra[0][:], extra[1][:])}
+        for g0, g1 in ((SPLIT, SPLIT + P), (SPLIT + P, G)):
+            cols = slice(g0 - SPLIT, g1 - SPLIT)
             nc.vector.quantize_mx(
                 out=late_codes[:, cols].bitcast(FP8X4),
                 scales=late_scales[:, cols],
-                in_=e_in[s].rearrange("p c t -> p (c t)"),
+                in_=bags(g0, g1).rearrange("p c t -> p (c t)"),
             )
-            e_mx.append((late_codes[:, cols], late_scales[:, cols]))
+            moving[(g0, g1)] = (late_codes[:, cols], late_scales[:, cols])
 
         result = keep.tile([P, STAGES, G], F32, name="result")
         out_rows = out.rearrange("(u p) g -> p u g", p=P)
@@ -160,39 +162,29 @@ def tile_attend_bag_bias_kernel(tc, xT, w, bias, offs, out):
                 stop=True,
             )
 
-        def empty(acc, u, c0, c1, on_vector):
-            dst, src, b = result[:, u, c0 * P : c1 * P], acc[:, 0 : (c1 - c0) * P], bias_cols[:, u : u + 1]
+        def store(u, g0, g1):
+            nc.sync.dma_start(out_rows[:, u, g0:g1], result[:, u, g0:g1])
+
+        def part(u, cuts, on_vector):
+            acc = psum.tile([P, 512], F32, name="acc")
+            first, end = cuts[0], cuts[-1]
+            for g0, g1 in zip(cuts, cuts[1:]):
+                multiply(acc[:, g0 - first : g1 - first], u, moving[(g0, g1)])
+            dst, src, b = result[:, u, first:end], acc[:, 0 : end - first], bias_cols[:, u : u + 1]
             if on_vector:
                 nc.vector.tensor_scalar(dst, src, b, None, ADD)
             else:
                 nc.scalar.activation(dst, src, IDENTITY, bias=b)
 
-        def store(u0, u1, c0, c1):
-            nc.sync.dma_start(out_rows[:, u0:u1, c0 * P : c1 * P], result[:, u0:u1, c0 * P : c1 * P])
-
-        def part(u, c0, c1, on_vector):
-            acc = psum.tile([P, 512], F32, name="acc")
-            if (c0, c1) == (2, 4):
-                multiply(acc[:, 0 : 2 * P], u, (late_codes[:], late_scales[:]))
-            elif (c0, c1) == (0, 2):
-                multiply(acc[:, 0 : 2 * P], u, early)
-            else:
-                for c in range(c0, c1):
-                    multiply(acc[:, (c - c0) * P : (c - c0 + 1) * P], u, e_mx[c])
-            empty(acc, u, c0, c1, on_vector)
-
-        part(0, 0, 1, False)
-        part(0, 1, 2, False)
-        store(0, 1, 0, 2)
+        part(0, (0, P), False)
+        part(0, (P, 2 * P), False)
+        store(0, 0, 2 * P)
         for u in range(1, STAGES):
-            part(u, 0, 2, False)
-            store(u, u + 1, 0, 2)
-        part(0, 2, 3, False)
-        part(0, 3, 4, True)
-        store(0, 1, 2, 4)
-        for u in range(1, 3):
-            part(u, 2, 4, u == 2)
-            store(u, u + 1, 2, 4)
-        part(3, 2, 3, False)
-        part(3, 3, 4, True)
-        store(3, 4, 2, 4)
+            part(u, (0, 2 * P, SPLIT), False)
+            store(u, 0, SPLIT)
+        part(0, (2 * P, SPLIT, SPLIT + P), False)
+        part(0, (SPLIT + P, G), True)
+        store(0, 2 * P, G)
+        for u in range(1, STAGES):
+            part(u, (SPLIT, SPLIT + P, G), u % 2 == 1)
+            store(u, SPLIT, G)

@@ -1,7 +1,6 @@
 from contextlib import ExitStack
 
 import concourse.mybir as mybir
-from concourse.masks import make_identity
 
 D, T, G, BAG, M = 512, 4096, 512, 2, 512
 FLOPS = 2 * D * M * G
@@ -13,13 +12,13 @@ U16 = mybir.dt.uint16
 U8 = mybir.dt.uint8
 FP8X4 = mybir.dt.float8_e4m3fn_x4
 ADD = mybir.AluOpType.add
+COPY = mybir.ActivationFunctionType.Copy
 IDENTITY = mybir.ActivationFunctionType.Identity
 
 P = 128
 PACK = 4
-STAGES = 4
-ENTRIES = P * BAG
-SPLIT = 320
+TILES = M // P
+HALF = P // 2
 
 
 def tile_attend_bag_bias_kernel(tc, xT, w, bias, offs, out):
@@ -29,74 +28,63 @@ def tile_attend_bag_bias_kernel(tc, xT, w, bias, offs, out):
         psum = ctx.enter_context(tc.psum_pool(name="psum", bufs=8))
 
         offsets = keep.tile([P, G * BAG // 16], U16, name="offsets")
-
+        bias_cols = keep.tile([P, 2, 2], F32, name="bias_cols")
+        planes = [keep.tile([P, T], F32, name="plane%d" % t) for t in range(PACK)]
+        w_raw = [keep.tile([P, PACK, 2 * P], F32, name="w_raw%d" % h, align_bytes=64) for h in range(2)]
         x_rows = xT.rearrange("(p t) c -> p t c", t=PACK)
-        pair = keep.tile([P, 2 * T], F32, name="pair")
-        nc.sync.dma_start(pair[:], xT.rearrange("(p h t) c -> p h (t c)", h=2, t=2)[:, 0, :])
-        nc.sync.dma_start(offsets[:], offs)
-        planes = [pair[:, 0:T], pair[:, T:]]
-        for t in range(2, PACK):
-            plane = keep.tile([P, T], F32, name="plane%d" % t)
-            nc.sync.dma_start(plane[:], x_rows[:, t, :])
-            planes.append(plane[:])
         w_rows = w.rearrange("(p t) m -> p t m", t=PACK)
-        w_raw = []
-        for u0, u1 in ((0, 2), (2, 3), (3, 4)):
-            raw = keep.tile([P, PACK, (u1 - u0) * P], F32, name="w_raw%d" % u0, align_bytes=64)
-            nc.sync.dma_start(raw[:], w_rows[:, :, u0 * P : u1 * P])
-            w_raw.extend(raw[:, :, i * P : (i + 1) * P] for i in range(u1 - u0))
+        nc.sync.dma_start(planes[0][:], x_rows[:, 0, :])
+        nc.sync.dma_start(offsets[:], offs)
+        for t in range(1, PACK):
+            nc.sync.dma_start(planes[t][:], x_rows[:, t, :])
+        for h in range(2):
+            nc.sync.dma_start(w_raw[h][:], w_rows[:, :, 2 * P * h : 2 * P * (h + 1)])
+        nc.sync.dma_start(bias_cols[:], bias.rearrange("(h p u) o -> p h (u o)", h=2, u=2))
 
-        bias_rows = keep.tile([P, P], F32, name="bias_rows")
-        nc.vector.memset(bias_rows[:], 0.0)
-        nc.scalar.dma_start(bias_rows[0:STAGES, :], bias.rearrange("(u p) o -> u (p o)", p=P))
-        ident = keep.tile([P, P], F32, name="ident")
-        make_identity(nc, ident[:])
-        turned = psum.tile([P, 512], F32, name="acc")
-        nc.tensor.transpose(turned[:, 0:P], bias_rows[:], ident[:])
-        bias_cols = keep.tile([P, STAGES], F32, name="bias_cols")
-        nc.scalar.activation(bias_cols[:], turned[:, 0:STAGES], IDENTITY)
-
-        grouped = keep.tile([P, 4 * P, PACK], BF16, name="grouped", align_bytes=64)
-        late_in = keep.tile([P, 2 * P, PACK], BF16, name="late_in", align_bytes=64)
-        w_in = [grouped[:, 0:P, :], grouped[:, 3 * P : 4 * P, :]]
-        for s in range(2, STAGES):
-            w_in.append(keep.tile([P, P, PACK], BF16, name="w_in%d" % s, align_bytes=64)[:])
+        grouped = keep.tile([P, 6 * P, PACK], BF16, name="grouped", align_bytes=64)
+        w_in = [grouped[:, 0:P, :], grouped[:, 2 * P : 3 * P, :]]
+        for u in range(2, TILES):
+            w_in.append(keep.tile([P, P, PACK], BF16, name="w_in%d" % u, align_bytes=64)[:])
 
         def bags(g0, g1):
-            if g0 < 2 * P:
-                return grouped[:, P + g0 : P + g1, :]
-            return late_in[:, g0 - 2 * P : g1 - 2 * P, :]
+            first = P if g0 < P else 2 * P
+            return grouped[:, first + g0 : first + g1, :]
 
-        e_in = [bags(c * P, (c + 1) * P) for c in range(STAGES)]
-        pool_runs = ((2 * P, SPLIT), (0, P), (P, 2 * P))
+        def gather(on_vector, picked, t, g0, g1):
+            window = planes[t][:].indirect(offsets[:, g0 * BAG // 16 : g1 * BAG // 16])
+            dst = picked[:, g0 * BAG : g1 * BAG]
+            if on_vector:
+                nc.vector.tensor_copy(dst, window)
+            else:
+                nc.scalar.activation(dst, window, COPY)
 
-        def gather(name, t, g0, g1, pool):
-            picked = pool.tile([P, (g1 - g0) * BAG], BF16, name=name)
-            nc.vector.tensor_copy(picked[:], planes[t].indirect(offsets[:, g0 * BAG // 16 : g1 * BAG // 16]))
-            return picked[:]
+        def add(on_vector, picked, t, g0, g1):
+            pairs = picked[:, g0 * BAG : g1 * BAG].rearrange("p (g j) -> p g j", j=BAG)
+            dst = bags(g0, g1)[:, :, t]
+            if on_vector:
+                with nc.allow_low_precision(reason="summed in float32, rounded once"):
+                    nc.vector.tensor_reduce(dst, pairs, mybir.AxisListType.X, ADD)
+            else:
+                nc.gpsimd.tensor_tensor(out=dst, in0=pairs[:, :, 0], in1=pairs[:, :, 1], op=ADD)
 
-        def add(engine, dst, entries):
-            pairs = entries.rearrange("p (g j) -> p j g", j=BAG)
-            engine.tensor_tensor(out=dst, in0=pairs[:, 0, :], in1=pairs[:, 1, :], op=ADD)
+        for t in range(PACK):
+            picked = keep.tile([P, G * BAG], BF16, name="picked%d" % t)
+            gather(True, picked, t, 0, HALF)
+            gather(False, picked, t, HALF, P)
+            gather(True, picked, t, P, 2 * P)
+            gather(False, picked, t, 2 * P, 3 * P)
+            gather(True, picked, t, 3 * P, 3 * P + HALF)
+            gather(False, picked, t, 3 * P + HALF, G)
+            for c in range(4):
+                add(c >= 2, picked, t, c * P, (c + 1) * P)
 
-        early = keep.tile([P, PACK - 1, G * BAG], F32, name="early")
-        for t in range(PACK - 1):
-            for runs in (((0, P), (P, 2 * P)), ((2 * P, G),)):
-                c0, c1 = runs[0][0] * BAG, runs[-1][1] * BAG
-                nc.vector.tensor_copy(early[:, t, c0:c1], planes[t].indirect(offsets[:, c0 // 16 : c1 // 16]))
-                for g0, g1 in runs:
-                    add(nc.gpsimd, bags(g0, g1)[:, :, t], early[:, t, g0 * BAG : g1 * BAG])
-
-        for g0, g1 in pool_runs:
-            add(nc.gpsimd, bags(g0, g1)[:, :, PACK - 1], gather("late%d" % g0, PACK - 1, g0, g1, keep))
-        late_second = gather("late_second", PACK - 1, SPLIT, G, keep)
-
-        def interleave(u):
-            nc.scalar.activation(
-                w_in[u].rearrange("p (c i) t -> p c t i", i=4),
-                w_raw[u].rearrange("p t (c i) -> p c t i", i=4),
-                IDENTITY,
-            )
+        def interleave(u, on_vector):
+            dst = w_in[u].rearrange("p (c i) t -> p c t i", i=2)
+            src = w_raw[u // 2][:].rearrange("p t (c i u) -> p u c t i", i=2, u=2)[:, u % 2, :, :, :]
+            if on_vector:
+                nc.vector.tensor_copy(dst, src)
+            else:
+                nc.scalar.activation(dst, src, COPY)
 
         def quantize(values, name, tag):
             width = values.shape[1]
@@ -107,84 +95,60 @@ def tile_attend_bag_bias_kernel(tc, xT, w, bias, offs, out):
             )
             return codes, scales
 
-        for u in range(STAGES):
-            interleave(u)
-        w_mx, e_mx = [], []
-
-        early_codes = keep.tile([P, 4 * P], U32, name="early_codes", align_bytes=64)
-        early_scales = keep.tile([P, 4 * P], U8, name="early_scales", align_bytes=64)
-        w_mx.extend((early_codes[:, c0 : c0 + P], early_scales[:, c0 : c0 + P]) for c0 in (0, 3 * P))
-        e_mx.extend((early_codes[:, c0 : c0 + P], early_scales[:, c0 : c0 + P]) for c0 in (P, 2 * P))
-        early = (early_codes[:, P : 3 * P], early_scales[:, P : 3 * P])
-
-        def quantize_pair(s):
-            cols = slice(2 * P * s, 2 * P * (s + 1))
-            nc.vector.quantize_mx(
-                out=early_codes[:, cols].bitcast(FP8X4),
-                scales=early_scales[:, cols],
-                in_=grouped[:, cols, :].rearrange("p c t -> p (c t)"),
-            )
-
-        quantize_pair(0)
-        quantize_pair(1)
-        extra = quantize(bags(2 * P, SPLIT), "extra", "w_raw0")
-        sums = w_raw[2][:, 0, 0 : (G - SPLIT) // 2].bitcast(BF16)
-        add(nc.vector, sums, late_second)
-        codes, scales = quantize(w_in[2], "w2", "codesw2")
-        w_mx.append((codes[:], scales[:]))
-        for g0, g1 in ((SPLIT, SPLIT + P), (SPLIT + P, G)):
-            nc.vector.tensor_copy(bags(g0, g1)[:, :, PACK - 1], sums[:, g0 - SPLIT : g1 - SPLIT])
-        codes, scales = quantize(w_in[3], "w3", "codesw3")
-        w_mx.append((codes[:], scales[:]))
-        late_codes = keep.tile([P, G - SPLIT], U32, name="late_codes", tag="w_raw3", align_bytes=64)
-        late_scales = keep.tile([P, G - SPLIT], U8, name="late_scales", align_bytes=64)
-        moving = {(0, P): e_mx[0], (P, 2 * P): e_mx[1], (0, 2 * P): early, (2 * P, SPLIT): (extra[0][:], extra[1][:])}
-        for g0, g1 in ((SPLIT, SPLIT + P), (SPLIT + P, G)):
-            cols = slice(g0 - SPLIT, g1 - SPLIT)
+        for u in range(3):
+            interleave(u, False)
+        late_codes = keep.tile([P, 2 * P], U32, name="late_codes", align_bytes=64)
+        late_scales = keep.tile([P, 2 * P], U8, name="late_scales", align_bytes=64)
+        w_mx, e_mx = [], {(2 * P, G): (late_codes[:], late_scales[:])}
+        for c in range(2, 4):
+            cols = slice((c - 2) * P, (c - 1) * P)
             nc.vector.quantize_mx(
                 out=late_codes[:, cols].bitcast(FP8X4),
                 scales=late_scales[:, cols],
-                in_=bags(g0, g1).rearrange("p c t -> p (c t)"),
+                in_=bags(c * P, (c + 1) * P).rearrange("p c t -> p (c t)"),
             )
-            moving[(g0, g1)] = (late_codes[:, cols], late_scales[:, cols])
+            e_mx[(c * P, (c + 1) * P)] = (late_codes[:, cols], late_scales[:, cols])
+        for s in range(2):
+            codes, scales = quantize(grouped[:, 2 * P * s : 2 * P * (s + 1), :], "pair%d" % s, "codespair%d" % s)
+            w_mx.append((codes[:, 0:P], scales[:, 0:P]))
+            e_mx[(P * s, P * (s + 1))] = (codes[:, P:], scales[:, P:])
+        interleave(3, True)
+        for u in range(2, TILES):
+            codes, scales = quantize(w_in[u], "w%d" % u, "codesw%d" % u)
+            w_mx.append((codes[:], scales[:]))
 
-        result = keep.tile([P, STAGES, G], F32, name="result")
-        out_rows = out.rearrange("(u p) g -> p u g", p=P)
-
-        def multiply(dst, u, moving):
-            nc.tensor.matmul_mx(
-                out=dst,
-                lhsT=w_mx[u][0].bitcast(FP8X4),
-                lhsT_scale=w_mx[u][1],
-                rhs=moving[0].bitcast(FP8X4),
-                rhs_scale=moving[1],
-                start=True,
-                stop=True,
-            )
-
-        def store(u, g0, g1):
-            nc.sync.dma_start(out_rows[:, u, g0:g1], result[:, u, g0:g1])
+        result = keep.tile([P, TILES, G], F32, name="result")
+        out_rows = out.rearrange("(h p u) g -> p h u g", h=2, u=2)
 
         def part(u, cuts, on_vector):
             acc = psum.tile([P, 512], F32, name="acc")
             first, end = cuts[0], cuts[-1]
             for g0, g1 in zip(cuts, cuts[1:]):
-                multiply(acc[:, g0 - first : g1 - first], u, moving[(g0, g1)])
-            dst, src, b = result[:, u, first:end], acc[:, 0 : end - first], bias_cols[:, u : u + 1]
+                nc.tensor.matmul_mx(
+                    out=acc[:, g0 - first : g1 - first],
+                    lhsT=w_mx[u][0].bitcast(FP8X4),
+                    lhsT_scale=w_mx[u][1],
+                    rhs=e_mx[(g0, g1)][0].bitcast(FP8X4),
+                    rhs_scale=e_mx[(g0, g1)][1],
+                    start=True,
+                    stop=True,
+                )
+            dst, src, b = result[:, u, first:end], acc[:, 0 : end - first], bias_cols[:, u // 2, u % 2 : u % 2 + 1]
             if on_vector:
                 nc.vector.tensor_scalar(dst, src, b, None, ADD)
             else:
                 nc.scalar.activation(dst, src, IDENTITY, bias=b)
 
-        part(0, (0, P), False)
-        part(0, (P, 2 * P), False)
-        store(0, 0, 2 * P)
-        for u in range(1, STAGES):
-            part(u, (0, 2 * P, SPLIT), False)
-            store(u, 0, SPLIT)
-        part(0, (2 * P, SPLIT, SPLIT + P), False)
-        part(0, (SPLIT + P, G), True)
-        store(0, 2 * P, G)
-        for u in range(1, STAGES):
-            part(u, (SPLIT, SPLIT + P, G), u % 2 == 1)
-            store(u, SPLIT, G)
+        def store(u, g0, g1):
+            nc.sync.dma_start(out_rows[:, u // 2, u % 2, g0:g1], result[:, u, g0:g1])
+
+        for u in range(TILES - 1):
+            part(u, (2 * P, G), False)
+            store(u, 2 * P, G)
+            part(u, (0, P, 2 * P), u > 0)
+            store(u, 0, 2 * P)
+        part(3, (2 * P, G), False)
+        store(3, 2 * P, G)
+        part(3, (0, P), True)
+        part(3, (P, 2 * P), False)
+        store(3, 0, 2 * P)

@@ -29,29 +29,30 @@ def tile_attend_bag_bias_kernel(tc, xT, w, bias, offs, out):
 
         offsets = keep.tile([P, G * BAG // 16], U16, name="offsets")
         bias_cols = keep.tile([P, 2, 2], F32, name="bias_cols")
-        planes = [keep.tile([P, T], F32, name="plane%d" % t) for t in range(PACK)]
+        planes = [keep.tile([P, T], F32, name="plane%d" % t)[:] for t in range(PACK)]
         w_raw = [keep.tile([P, PACK, 2 * P], F32, name="w_raw%d" % h, align_bytes=64) for h in range(2)]
         x_rows = xT.rearrange("(p t) c -> p t c", t=PACK)
         w_rows = w.rearrange("(p t) m -> p t m", t=PACK)
-        nc.sync.dma_start(planes[0][:], x_rows[:, 0, :])
+        nc.sync.dma_start(planes[0], x_rows[:, 0, :])
         nc.sync.dma_start(offsets[:], offs)
         for t in range(1, PACK):
-            nc.sync.dma_start(planes[t][:], x_rows[:, t, :])
+            nc.sync.dma_start(planes[t], x_rows[:, t, :])
         for h in range(2):
             nc.sync.dma_start(w_raw[h][:], w_rows[:, :, 2 * P * h : 2 * P * (h + 1)])
         nc.sync.dma_start(bias_cols[:], bias.rearrange("(h p u) o -> p h (u o)", h=2, u=2))
 
         grouped = keep.tile([P, 6 * P, PACK], BF16, name="grouped", align_bytes=64)
-        w_in = [grouped[:, 0:P, :], grouped[:, 2 * P : 3 * P, :]]
-        for u in range(2, TILES):
-            w_in.append(keep.tile([P, P, PACK], BF16, name="w_in%d" % u, align_bytes=64)[:])
-
-        def bags(g0, g1):
-            first = P if g0 < P else 2 * P
-            return grouped[:, first + g0 : first + g1, :]
+        codes = keep.tile([P, 6 * P], U32, name="codes", align_bytes=64)
+        scales = keep.tile([P, 6 * P], U8, name="scales", align_bytes=64)
+        late_in = keep.tile([P, 2 * P, PACK], BF16, name="late_in", align_bytes=64)
+        late_codes = keep.tile([P, 2 * P], U32, name="late_codes", align_bytes=64)
+        late_scales = keep.tile([P, 2 * P], U8, name="late_scales", align_bytes=64)
+        w_in = [grouped[:, 0:P, :], grouped[:, 5 * P :, :], late_in[:, 0:P, :], late_in[:, P:, :]]
+        w_mx = [(codes[:, c : c + P], scales[:, c : c + P]) for c in (0, 5 * P)]
+        w_mx.extend((late_codes[:, c : c + P], late_scales[:, c : c + P]) for c in (0, P))
 
         def gather(on_vector, picked, t, g0, g1):
-            window = planes[t][:].indirect(offsets[:, g0 * BAG // 16 : g1 * BAG // 16])
+            window = planes[t].indirect(offsets[:, g0 * BAG // 16 : g1 * BAG // 16])
             dst = picked[:, g0 * BAG : g1 * BAG]
             if on_vector:
                 nc.vector.tensor_copy(dst, window)
@@ -60,7 +61,7 @@ def tile_attend_bag_bias_kernel(tc, xT, w, bias, offs, out):
 
         def add(on_vector, picked, t, g0, g1):
             pairs = picked[:, g0 * BAG : g1 * BAG].rearrange("p (g j) -> p g j", j=BAG)
-            dst = bags(g0, g1)[:, :, t]
+            dst = grouped[:, P + g0 : P + g1, t]
             if on_vector:
                 with nc.allow_low_precision(reason="summed in float32, rounded once"):
                     nc.vector.tensor_reduce(dst, pairs, mybir.AxisListType.X, ADD)
@@ -86,36 +87,20 @@ def tile_attend_bag_bias_kernel(tc, xT, w, bias, offs, out):
             else:
                 nc.scalar.activation(dst, src, COPY)
 
-        def quantize(values, name, tag):
-            width = values.shape[1]
-            codes = keep.tile([P, width], U32, name="codes" + name, tag=tag, align_bytes=64)
-            scales = keep.tile([P, width], U8, name="scales" + name, align_bytes=64)
+        def quantize(values, words, plane, c0, c1):
             nc.vector.quantize_mx(
-                out=codes[:].bitcast(FP8X4), scales=scales[:], in_=values.rearrange("p c t -> p (c t)")
+                out=words[:, c0:c1].bitcast(FP8X4),
+                scales=plane[:, c0:c1],
+                in_=values[:, c0:c1, :].rearrange("p c t -> p (c t)"),
             )
-            return codes, scales
 
         for u in range(3):
             interleave(u, False)
-        late_codes = keep.tile([P, 2 * P], U32, name="late_codes", align_bytes=64)
-        late_scales = keep.tile([P, 2 * P], U8, name="late_scales", align_bytes=64)
-        w_mx, e_mx = [], {(2 * P, G): (late_codes[:], late_scales[:])}
-        for c in range(2, 4):
-            cols = slice((c - 2) * P, (c - 1) * P)
-            nc.vector.quantize_mx(
-                out=late_codes[:, cols].bitcast(FP8X4),
-                scales=late_scales[:, cols],
-                in_=bags(c * P, (c + 1) * P).rearrange("p c t -> p (c t)"),
-            )
-            e_mx[(c * P, (c + 1) * P)] = (late_codes[:, cols], late_scales[:, cols])
-        for s in range(2):
-            codes, scales = quantize(grouped[:, 2 * P * s : 2 * P * (s + 1), :], "pair%d" % s, "codespair%d" % s)
-            w_mx.append((codes[:, 0:P], scales[:, 0:P]))
-            e_mx[(P * s, P * (s + 1))] = (codes[:, P:], scales[:, P:])
+        for c0, c1 in ((3 * P, 4 * P), (2 * P, 3 * P), (0, 2 * P), (4 * P, 6 * P)):
+            quantize(grouped, codes, scales, c0, c1)
         interleave(3, True)
-        for u in range(2, TILES):
-            codes, scales = quantize(w_in[u], "w%d" % u, "codesw%d" % u)
-            w_mx.append((codes[:], scales[:]))
+        for c0 in (0, P):
+            quantize(late_in, late_codes, late_scales, c0, c0 + P)
 
         result = keep.tile([P, TILES, G], F32, name="result")
         out_rows = out.rearrange("(h p u) g -> p h u g", h=2, u=2)
@@ -128,8 +113,8 @@ def tile_attend_bag_bias_kernel(tc, xT, w, bias, offs, out):
                     out=acc[:, g0 - first : g1 - first],
                     lhsT=w_mx[u][0].bitcast(FP8X4),
                     lhsT_scale=w_mx[u][1],
-                    rhs=e_mx[(g0, g1)][0].bitcast(FP8X4),
-                    rhs_scale=e_mx[(g0, g1)][1],
+                    rhs=codes[:, P + g0 : P + g1].bitcast(FP8X4),
+                    rhs_scale=scales[:, P + g0 : P + g1],
                     start=True,
                     stop=True,
                 )
@@ -142,13 +127,18 @@ def tile_attend_bag_bias_kernel(tc, xT, w, bias, offs, out):
         def store(u, g0, g1):
             nc.sync.dma_start(out_rows[:, u // 2, u % 2, g0:g1], result[:, u, g0:g1])
 
-        for u in range(TILES - 1):
-            part(u, (2 * P, G), False)
-            store(u, 2 * P, G)
-            part(u, (0, P, 2 * P), u > 0)
+        part(0, (0, P), False)
+        store(0, 0, P)
+        part(0, (P, 2 * P), False)
+        store(0, P, 2 * P)
+        part(0, (2 * P, 3 * P, G), False)
+        store(0, 2 * P, G)
+        for u in range(1, 3):
+            part(u, (0, 2 * P), False)
             store(u, 0, 2 * P)
-        part(3, (2 * P, G), False)
-        store(3, 2 * P, G)
-        part(3, (0, P), True)
-        part(3, (P, 2 * P), False)
-        store(3, 0, 2 * P)
+            part(u, (2 * P, G), True)
+            store(u, 2 * P, G)
+        part(3, (0, 2 * P), False)
+        part(3, (2 * P, 3 * P), True)
+        part(3, (3 * P, G), False)
+        store(3, 0, G)

@@ -1,6 +1,7 @@
 from contextlib import ExitStack
 
 import concourse.mybir as mybir
+from concourse.masks import make_identity
 
 D, T, G, BAG, M = 512, 4096, 512, 2, 512
 FLOPS = 2 * D * M * G
@@ -28,18 +29,28 @@ def tile_attend_bag_bias_kernel(tc, xT, w, bias, offs, out):
         psum = ctx.enter_context(tc.psum_pool(name="psum", bufs=8))
 
         offsets = keep.tile([P, G * BAG // 16], U16, name="offsets")
-        bias_cols = keep.tile([P, 2, 2], F32, name="bias_cols")
+        bias_rows = keep.tile([P, P], F32, name="bias_rows")
+        nc.vector.memset(bias_rows[:], 0.0)
         planes = [keep.tile([P, T], F32, name="plane%d" % t)[:] for t in range(PACK)]
-        w_raw = [keep.tile([P, PACK, 2 * P], F32, name="w_raw%d" % h, align_bytes=64) for h in range(2)]
         x_rows = xT.rearrange("(p t) c -> p t c", t=PACK)
         w_rows = w.rearrange("(p t) m -> p t m", t=PACK)
         nc.sync.dma_start(planes[0], x_rows[:, 0, :])
+        nc.sync.dma_start(bias_rows[0:TILES, :], bias.rearrange("(u p) o -> u (p o)", p=P))
         nc.sync.dma_start(offsets[:], offs)
         for t in range(1, PACK):
             nc.sync.dma_start(planes[t], x_rows[:, t, :])
-        for h in range(2):
-            nc.sync.dma_start(w_raw[h][:], w_rows[:, :, 2 * P * h : 2 * P * (h + 1)])
-        nc.sync.dma_start(bias_cols[:], bias.rearrange("(h p u) o -> p h (u o)", h=2, u=2))
+        w_raw = []
+        for u0, u1 in ((0, 2), (2, 3), (3, 4)):
+            raw = keep.tile([P, PACK, (u1 - u0) * P], F32, name="w_raw%d" % u0, align_bytes=64)
+            nc.sync.dma_start(raw[:], w_rows[:, :, u0 * P : u1 * P])
+            w_raw.extend(raw[:, :, i * P : (i + 1) * P] for i in range(u1 - u0))
+
+        ident = keep.tile([P, P], F32, name="ident")
+        make_identity(nc, ident[:])
+        turned = psum.tile([P, 512], F32, name="acc")
+        nc.tensor.transpose(turned[:, 0:P], bias_rows[:], ident[:])
+        bias_cols = keep.tile([P, TILES], F32, name="bias_cols")
+        nc.scalar.activation(bias_cols[:], turned[:, 0:TILES], IDENTITY)
 
         grouped = keep.tile([P, 6 * P, PACK], BF16, name="grouped", align_bytes=64)
         codes = keep.tile([P, 6 * P], U32, name="codes", align_bytes=64)
@@ -80,8 +91,8 @@ def tile_attend_bag_bias_kernel(tc, xT, w, bias, offs, out):
                 add(c >= 2, picked, t, c * P, (c + 1) * P)
 
         def interleave(u, on_vector):
-            dst = w_in[u].rearrange("p (c i) t -> p c t i", i=2)
-            src = w_raw[u // 2][:].rearrange("p t (c i u) -> p u c t i", i=2, u=2)[:, u % 2, :, :, :]
+            dst = w_in[u].rearrange("p (c i) t -> p c t i", i=4)
+            src = w_raw[u].rearrange("p t (c i) -> p c t i", i=4)
             if on_vector:
                 nc.vector.tensor_copy(dst, src)
             else:
@@ -98,12 +109,12 @@ def tile_attend_bag_bias_kernel(tc, xT, w, bias, offs, out):
             interleave(u, False)
         for c0, c1 in ((3 * P, 4 * P), (2 * P, 3 * P), (0, 2 * P), (4 * P, 6 * P)):
             quantize(grouped, codes, scales, c0, c1)
+        quantize(late_in, late_codes, late_scales, 0, P)
         interleave(3, True)
-        for c0 in (0, P):
-            quantize(late_in, late_codes, late_scales, c0, c0 + P)
+        quantize(late_in, late_codes, late_scales, P, 2 * P)
 
         result = keep.tile([P, TILES, G], F32, name="result")
-        out_rows = out.rearrange("(h p u) g -> p h u g", h=2, u=2)
+        out_rows = out.rearrange("(u p) g -> p u g", p=P)
 
         def part(u, cuts, on_vector):
             acc = psum.tile([P, 512], F32, name="acc")
@@ -118,19 +129,18 @@ def tile_attend_bag_bias_kernel(tc, xT, w, bias, offs, out):
                     start=True,
                     stop=True,
                 )
-            dst, src, b = result[:, u, first:end], acc[:, 0 : end - first], bias_cols[:, u // 2, u % 2 : u % 2 + 1]
+            dst, src, b = result[:, u, first:end], acc[:, 0 : end - first], bias_cols[:, u : u + 1]
             if on_vector:
                 nc.vector.tensor_scalar(dst, src, b, None, ADD)
             else:
                 nc.scalar.activation(dst, src, IDENTITY, bias=b)
 
         def store(u, g0, g1):
-            nc.sync.dma_start(out_rows[:, u // 2, u % 2, g0:g1], result[:, u, g0:g1])
+            nc.sync.dma_start(out_rows[:, u, g0:g1], result[:, u, g0:g1])
 
         part(0, (0, P), False)
-        store(0, 0, P)
         part(0, (P, 2 * P), False)
-        store(0, P, 2 * P)
+        store(0, 0, 2 * P)
         part(0, (2 * P, 3 * P, G), False)
         store(0, 2 * P, G)
         for u in range(1, 3):

@@ -31,16 +31,18 @@ def tile_attend_bag_bias_kernel(tc, xT, w, bias, offs, out):
         offsets = keep.tile([P, G * BAG // 16], U16, name="offsets")
         bias_rows = keep.tile([P, P], F32, name="bias_rows")
         nc.vector.memset(bias_rows[:], 0.0)
-        planes = [keep.tile([P, T], F32, name="plane%d" % t)[:] for t in range(PACK)]
+        pair = keep.tile([P, 2 * T], F32, name="pair")
+        planes = [pair[:, 0:T], pair[:, T:]]
+        planes.extend(keep.tile([P, T], F32, name="plane%d" % t)[:] for t in range(2, PACK))
         x_rows = xT.rearrange("(p t) c -> p t c", t=PACK)
         w_rows = w.rearrange("(p t) m -> p t m", t=PACK)
-        nc.sync.dma_start(planes[0], x_rows[:, 0, :])
+        nc.sync.dma_start(pair[:], xT.rearrange("(p h t) c -> p h (t c)", h=2, t=2)[:, 0, :])
         nc.sync.dma_start(bias_rows[0:TILES, :], bias.rearrange("(u p) o -> u (p o)", p=P))
         nc.sync.dma_start(offsets[:], offs)
-        for t in range(1, PACK):
+        for t in range(2, PACK):
             nc.sync.dma_start(planes[t], x_rows[:, t, :])
         w_raw = []
-        for u0, u1 in ((0, 2), (2, 3), (3, 4)):
+        for u0, u1 in ((0, 1), (1, 3), (3, 4)):
             raw = keep.tile([P, PACK, (u1 - u0) * P], F32, name="w_raw%d" % u0, align_bytes=64)
             nc.sync.dma_start(raw[:], w_rows[:, :, u0 * P : u1 * P])
             w_raw.extend(raw[:, :, i * P : (i + 1) * P] for i in range(u1 - u0))
@@ -52,14 +54,15 @@ def tile_attend_bag_bias_kernel(tc, xT, w, bias, offs, out):
         bias_cols = keep.tile([P, TILES], F32, name="bias_cols")
         nc.scalar.activation(bias_cols[:], turned[:, 0:TILES], IDENTITY)
 
-        grouped = keep.tile([P, 6 * P, PACK], BF16, name="grouped", align_bytes=64)
-        codes = keep.tile([P, 6 * P], U32, name="codes", align_bytes=64)
-        scales = keep.tile([P, 6 * P], U8, name="scales", align_bytes=64)
-        late_in = keep.tile([P, 2 * P, PACK], BF16, name="late_in", align_bytes=64)
+        grouped = keep.tile([P, 4 * P, PACK], BF16, name="grouped", align_bytes=64)
+        codes = keep.tile([P, 4 * P], U32, name="codes", align_bytes=64)
+        scales = keep.tile([P, 4 * P], U8, name="scales", align_bytes=64)
+        high_in = keep.tile([P, 2 * P, PACK], BF16, name="high_in", align_bytes=64)
+        third_in = keep.tile([P, P, PACK], BF16, name="third_in", align_bytes=64)
         late_codes = keep.tile([P, 2 * P], U32, name="late_codes", align_bytes=64)
         late_scales = keep.tile([P, 2 * P], U8, name="late_scales", align_bytes=64)
-        w_in = [grouped[:, 0:P, :], grouped[:, 5 * P :, :], late_in[:, 0:P, :], late_in[:, P:, :]]
-        w_mx = [(codes[:, c : c + P], scales[:, c : c + P]) for c in (0, 5 * P)]
+        w_in = [grouped[:, 0:P, :], grouped[:, 3 * P :, :], third_in[:]]
+        w_mx = [(codes[:, c : c + P], scales[:, c : c + P]) for c in (0, 3 * P)]
         w_mx.extend((late_codes[:, c : c + P], late_scales[:, c : c + P]) for c in (0, P))
 
         def gather(on_vector, picked, t, g0, g1):
@@ -72,23 +75,29 @@ def tile_attend_bag_bias_kernel(tc, xT, w, bias, offs, out):
 
         def add(on_vector, picked, t, g0, g1):
             pairs = picked[:, g0 * BAG : g1 * BAG].rearrange("p (g j) -> p g j", j=BAG)
-            dst = grouped[:, P + g0 : P + g1, t]
+            dst = grouped[:, P + g0 : P + g1, t] if g0 < 2 * P else high_in[:, g0 - 2 * P : g1 - 2 * P, t]
             if on_vector:
                 with nc.allow_low_precision(reason="summed in float32, rounded once"):
                     nc.vector.tensor_reduce(dst, pairs, mybir.AxisListType.X, ADD)
             else:
                 nc.gpsimd.tensor_tensor(out=dst, in0=pairs[:, :, 0], in1=pairs[:, :, 1], op=ADD)
 
-        for t in range(PACK):
-            picked = keep.tile([P, G * BAG], BF16, name="picked%d" % t)
-            gather(True, picked, t, 0, HALF)
-            gather(False, picked, t, HALF, P)
-            gather(True, picked, t, P, 2 * P)
-            gather(False, picked, t, 2 * P, 3 * P)
-            gather(True, picked, t, 3 * P, 3 * P + HALF)
-            gather(False, picked, t, 3 * P + HALF, G)
-            for c in range(4):
-                add(c >= 2, picked, t, c * P, (c + 1) * P)
+        last = PACK - 1
+        for t in range(last):
+            picked = keep.tile([P, G * BAG], F32 if t < 2 else BF16, name="picked%d" % t)
+            for h in range(2):
+                gather(t < 2, picked, t, 2 * P * h, 2 * P * (h + 1))
+                for c in range(2 * h, 2 * h + 2):
+                    add(c % 2 == 1, picked, t, c * P, (c + 1) * P)
+        picked = keep.tile([P, G * BAG], BF16, name="picked3")
+        gather(True, picked, last, 0, HALF)
+        gather(False, picked, last, HALF, P)
+        gather(True, picked, last, 2 * P, 3 * P)
+        gather(False, picked, last, 3 * P, G)
+        gather(True, picked, last, P, P + HALF)
+        gather(False, picked, last, P + HALF, 2 * P)
+        for c in (0, 2, 3, 1):
+            add(c % 2 == 1, picked, last, c * P, (c + 1) * P)
 
         def interleave(u, on_vector):
             dst = w_in[u].rearrange("p (c i) t -> p c t i", i=4)
@@ -107,42 +116,63 @@ def tile_attend_bag_bias_kernel(tc, xT, w, bias, offs, out):
 
         for u in range(3):
             interleave(u, False)
-        for c0, c1 in ((3 * P, 4 * P), (2 * P, 3 * P), (0, 2 * P), (4 * P, 6 * P)):
-            quantize(grouped, codes, scales, c0, c1)
-        quantize(late_in, late_codes, late_scales, 0, P)
+        quantize(grouped, codes, scales, 0, 2 * P)
+        high_codes = keep.tile([P, 2 * P], U32, name="high_codes", tag="w_raw0", align_bytes=64)
+        high_scales = keep.tile([P, 2 * P], U8, name="high_scales", align_bytes=64)
+        for c0 in (P, 0):
+            quantize(high_in, high_codes, high_scales, c0, c0 + P)
+        quantize(grouped, codes, scales, 2 * P, 4 * P)
+        quantize(third_in, late_codes, late_scales, 0, P)
+        fourth_in = keep.tile([P, 2 * P, PACK], BF16, name="fourth_in", tag="w_raw1", align_bytes=64)
+        w_in.append(fourth_in[:, P:, :])
         interleave(3, True)
-        quantize(late_in, late_codes, late_scales, P, 2 * P)
+        quantize(fourth_in, late_codes, late_scales, P, 2 * P)
 
-        result = keep.tile([P, TILES, G], F32, name="result")
+        result = keep.tile([P, TILES - 1, G], F32, name="result")
+        reused = keep.tile([P, 2 * G], F32, name="reused", tag="w_raw1", align_bytes=64)
+
+        def staged(u, g0, g1):
+            if u == 3:
+                return reused[:, G + g0 : G + g1]
+            if u > 0 and g0 >= 2 * P:
+                return reused[:, 2 * P * (u - 2) + g0 : 2 * P * (u - 2) + g1]
+            return result[:, u, g0:g1]
+
         out_rows = out.rearrange("(u p) g -> p u g", p=P)
 
         def part(u, cuts, on_vector):
             acc = psum.tile([P, 512], F32, name="acc")
             first, end = cuts[0], cuts[-1]
             for g0, g1 in zip(cuts, cuts[1:]):
+                if g0 < 2 * P:
+                    moving = (codes[:, P + g0 : P + g1], scales[:, P + g0 : P + g1])
+                else:
+                    moving = (high_codes[:, g0 - 2 * P : g1 - 2 * P], high_scales[:, g0 - 2 * P : g1 - 2 * P])
                 nc.tensor.matmul_mx(
                     out=acc[:, g0 - first : g1 - first],
                     lhsT=w_mx[u][0].bitcast(FP8X4),
                     lhsT_scale=w_mx[u][1],
-                    rhs=codes[:, P + g0 : P + g1].bitcast(FP8X4),
-                    rhs_scale=scales[:, P + g0 : P + g1],
+                    rhs=moving[0].bitcast(FP8X4),
+                    rhs_scale=moving[1],
                     start=True,
                     stop=True,
                 )
-            dst, src, b = result[:, u, first:end], acc[:, 0 : end - first], bias_cols[:, u : u + 1]
+            dst, src, b = staged(u, first, end), acc[:, 0 : end - first], bias_cols[:, u : u + 1]
             if on_vector:
                 nc.vector.tensor_scalar(dst, src, b, None, ADD)
             else:
                 nc.scalar.activation(dst, src, IDENTITY, bias=b)
 
         def store(u, g0, g1):
-            nc.sync.dma_start(out_rows[:, u, g0:g1], result[:, u, g0:g1])
+            nc.sync.dma_start(out_rows[:, u, g0:g1], staged(u, g0, g1))
 
         part(0, (0, P), False)
-        part(0, (P, 2 * P), False)
-        store(0, 0, 2 * P)
-        part(0, (2 * P, 3 * P, G), False)
+        store(0, 0, P)
+        part(0, (3 * P, G), False)
+        part(0, (2 * P, 3 * P), False)
         store(0, 2 * P, G)
+        part(0, (P, 2 * P), False)
+        store(0, P, 2 * P)
         for u in range(1, 3):
             part(u, (0, 2 * P), False)
             store(u, 0, 2 * P)

@@ -42,7 +42,7 @@ def tile_attend_bag_bias_kernel(tc, xT, w, bias, offs, out):
         for t in range(2, PACK):
             nc.sync.dma_start(planes[t], x_rows[:, t, :])
         w_raw = []
-        for u0, u1 in ((0, 1), (1, 3), (3, 4)):
+        for u0, u1 in ((0, 1), (1, 2), (2, 3), (3, 4)):
             raw = keep.tile([P, PACK, (u1 - u0) * P], F32, name="w_raw%d" % u0, align_bytes=64)
             nc.sync.dma_start(raw[:], w_rows[:, :, u0 * P : u1 * P])
             w_raw.extend(raw[:, :, i * P : (i + 1) * P] for i in range(u1 - u0))
@@ -58,10 +58,9 @@ def tile_attend_bag_bias_kernel(tc, xT, w, bias, offs, out):
         codes = keep.tile([P, 4 * P], U32, name="codes", align_bytes=64)
         scales = keep.tile([P, 4 * P], U8, name="scales", align_bytes=64)
         high_in = keep.tile([P, 2 * P, PACK], BF16, name="high_in", align_bytes=64)
-        third_in = keep.tile([P, P, PACK], BF16, name="third_in", align_bytes=64)
         late_codes = keep.tile([P, 2 * P], U32, name="late_codes", align_bytes=64)
         late_scales = keep.tile([P, 2 * P], U8, name="late_scales", align_bytes=64)
-        w_in = [grouped[:, 0:P, :], grouped[:, 3 * P :, :], third_in[:]]
+        w_in = [grouped[:, 0:P, :], grouped[:, 3 * P :, :]]
         w_mx = [(codes[:, c : c + P], scales[:, c : c + P]) for c in (0, 3 * P)]
         w_mx.extend((late_codes[:, c : c + P], late_scales[:, c : c + P]) for c in (0, P))
 
@@ -89,15 +88,12 @@ def tile_attend_bag_bias_kernel(tc, xT, w, bias, offs, out):
                 gather(t < 2, picked, t, 2 * P * h, 2 * P * (h + 1))
                 for c in range(2 * h, 2 * h + 2):
                     add(c % 2 == 1, picked, t, c * P, (c + 1) * P)
-        picked = keep.tile([P, G * BAG], BF16, name="picked3")
-        gather(True, picked, last, 0, HALF)
-        gather(False, picked, last, HALF, P)
-        gather(True, picked, last, 2 * P, 3 * P)
-        gather(False, picked, last, 3 * P, G)
-        gather(True, picked, last, P, P + HALF)
-        gather(False, picked, last, P + HALF, 2 * P)
+        wide = keep.tile([P, G * BAG], F32, name="wide")
+        narrow = keep.tile([P, G * BAG], BF16, name="narrow")
+        for c in (0, 3, 2, 1):
+            gather(c % 2 == 0, narrow if c % 2 else wide, last, c * P, (c + 1) * P)
         for c in (0, 2, 3, 1):
-            add(c % 2 == 1, picked, last, c * P, (c + 1) * P)
+            add(c % 2 == 1, narrow if c % 2 else wide, last, c * P, (c + 1) * P)
 
         def interleave(u, on_vector):
             dst = w_in[u].rearrange("p (c i) t -> p c t i", i=4)
@@ -114,6 +110,8 @@ def tile_attend_bag_bias_kernel(tc, xT, w, bias, offs, out):
                 in_=values[:, c0:c1, :].rearrange("p c t -> p (c t)"),
             )
 
+        third_in = keep.tile([P, P, PACK], BF16, name="third_in", align_bytes=64)
+        w_in.append(third_in[:])
         for u in range(3):
             interleave(u, False)
         quantize(grouped, codes, scales, 0, 2 * P)
@@ -123,19 +121,17 @@ def tile_attend_bag_bias_kernel(tc, xT, w, bias, offs, out):
             quantize(high_in, high_codes, high_scales, c0, c0 + P)
         quantize(grouped, codes, scales, 2 * P, 4 * P)
         quantize(third_in, late_codes, late_scales, 0, P)
-        fourth_in = keep.tile([P, 2 * P, PACK], BF16, name="fourth_in", tag="w_raw1", align_bytes=64)
+        fourth_in = keep.tile([P, 2 * P, PACK], BF16, name="fourth_in", tag="w_raw2", align_bytes=64)
         w_in.append(fourth_in[:, P:, :])
         interleave(3, True)
         quantize(fourth_in, late_codes, late_scales, P, 2 * P)
 
-        result = keep.tile([P, TILES - 1, G], F32, name="result")
-        reused = keep.tile([P, 2 * G], F32, name="reused", tag="w_raw1", align_bytes=64)
+        result = keep.tile([P, 2, G], F32, name="result")
+        reused = keep.tile([P, TILES - 1, G], F32, name="reused", tag="w_raw2", align_bytes=64)
 
         def staged(u, g0, g1):
-            if u == 3:
-                return reused[:, G + g0 : G + g1]
-            if u > 0 and g0 >= 2 * P:
-                return reused[:, 2 * P * (u - 2) + g0 : 2 * P * (u - 2) + g1]
+            if u > 1 or u == 1 and g0 >= 2 * P:
+                return reused[:, u - 1, g0:g1]
             return result[:, u, g0:g1]
 
         out_rows = out.rearrange("(u p) g -> p u g", p=P)
@@ -173,12 +169,11 @@ def tile_attend_bag_bias_kernel(tc, xT, w, bias, offs, out):
         store(0, 2 * P, G)
         part(0, (P, 2 * P), False)
         store(0, P, 2 * P)
-        for u in range(1, 3):
+        for h in range(2):
+            part(1, (2 * P * h, 2 * P * (h + 1)), h == 1)
+            store(1, 2 * P * h, 2 * P * (h + 1))
+        for u in range(2, TILES):
             part(u, (0, 2 * P), False)
-            store(u, 0, 2 * P)
-            part(u, (2 * P, G), True)
-            store(u, 2 * P, G)
-        part(3, (0, 2 * P), False)
-        part(3, (2 * P, 3 * P), True)
-        part(3, (3 * P, G), False)
-        store(3, 0, G)
+            part(u, (2 * P, 3 * P), True)
+            part(u, (3 * P, G), u == 2)
+            store(u, 0, G)

@@ -19,7 +19,6 @@ IDENTITY = mybir.ActivationFunctionType.Identity
 P = 128
 PACK = 4
 TILES = M // P
-HALF = P // 2
 
 
 def tile_attend_bag_bias_kernel(tc, xT, w, bias, offs, out):
@@ -42,10 +41,10 @@ def tile_attend_bag_bias_kernel(tc, xT, w, bias, offs, out):
         for t in range(2, PACK):
             nc.sync.dma_start(planes[t], x_rows[:, t, :])
         w_raw = []
-        for u0, u1 in ((0, 1), (1, 2), (2, 3), (3, 4)):
-            raw = keep.tile([P, PACK, (u1 - u0) * P], F32, name="w_raw%d" % u0, align_bytes=64)
-            nc.sync.dma_start(raw[:], w_rows[:, :, u0 * P : u1 * P])
-            w_raw.extend(raw[:, :, i * P : (i + 1) * P] for i in range(u1 - u0))
+        for u in range(TILES):
+            raw = keep.tile([P, PACK, P], F32, name="w_raw%d" % u, align_bytes=64)
+            nc.sync.dma_start(raw[:], w_rows[:, :, u * P : (u + 1) * P])
+            w_raw.append(raw)
 
         ident = keep.tile([P, P], F32, name="ident")
         make_identity(nc, ident[:])
@@ -54,15 +53,7 @@ def tile_attend_bag_bias_kernel(tc, xT, w, bias, offs, out):
         bias_cols = keep.tile([P, TILES], F32, name="bias_cols")
         nc.scalar.activation(bias_cols[:], turned[:, 0:TILES], IDENTITY)
 
-        grouped = keep.tile([P, 4 * P, PACK], BF16, name="grouped", align_bytes=64)
-        codes = keep.tile([P, 4 * P], U32, name="codes", align_bytes=64)
-        scales = keep.tile([P, 4 * P], U8, name="scales", align_bytes=64)
-        high_in = keep.tile([P, 2 * P, PACK], BF16, name="high_in", align_bytes=64)
-        late_codes = keep.tile([P, 2 * P], U32, name="late_codes", align_bytes=64)
-        late_scales = keep.tile([P, 2 * P], U8, name="late_scales", align_bytes=64)
-        w_in = [grouped[:, 0:P, :], grouped[:, 3 * P :, :]]
-        w_mx = [(codes[:, c : c + P], scales[:, c : c + P]) for c in (0, 3 * P)]
-        w_mx.extend((late_codes[:, c : c + P], late_scales[:, c : c + P]) for c in (0, P))
+        grouped = keep.tile([P, P + G, PACK], BF16, name="grouped", align_bytes=64)
 
         def gather(on_vector, picked, t, g0, g1):
             window = planes[t].indirect(offsets[:, g0 * BAG // 16 : g1 * BAG // 16])
@@ -72,10 +63,10 @@ def tile_attend_bag_bias_kernel(tc, xT, w, bias, offs, out):
             else:
                 nc.scalar.activation(dst, window, COPY)
 
-        def add(on_vector, picked, t, g0, g1):
-            pairs = picked[:, g0 * BAG : g1 * BAG].rearrange("p (g j) -> p g j", j=BAG)
-            dst = grouped[:, P + g0 : P + g1, t] if g0 < 2 * P else high_in[:, g0 - 2 * P : g1 - 2 * P, t]
-            if on_vector:
+        def add(picked, t, c):
+            pairs = picked[:, c * P * BAG : (c + 1) * P * BAG].rearrange("p (g j) -> p g j", j=BAG)
+            dst = grouped[:, (c + 1) * P : (c + 2) * P, t]
+            if c % 2 == 1:
                 with nc.allow_low_precision(reason="summed in float32, rounded once"):
                     nc.vector.tensor_reduce(dst, pairs, mybir.AxisListType.X, ADD)
             else:
@@ -87,65 +78,66 @@ def tile_attend_bag_bias_kernel(tc, xT, w, bias, offs, out):
             for h in range(2):
                 gather(t < 2, picked, t, 2 * P * h, 2 * P * (h + 1))
                 for c in range(2 * h, 2 * h + 2):
-                    add(c % 2 == 1, picked, t, c * P, (c + 1) * P)
+                    add(picked, t, c)
         wide = keep.tile([P, G * BAG], F32, name="wide")
         narrow = keep.tile([P, G * BAG], BF16, name="narrow")
-        for c in (0, 3, 2, 1):
+        for c in range(4):
             gather(c % 2 == 0, narrow if c % 2 else wide, last, c * P, (c + 1) * P)
-        for c in (0, 2, 3, 1):
-            add(c % 2 == 1, narrow if c % 2 else wide, last, c * P, (c + 1) * P)
+        for c in range(4):
+            add(narrow if c % 2 else wide, last, c)
 
-        def interleave(u, on_vector):
-            dst = w_in[u].rearrange("p (c i) t -> p c t i", i=4)
-            src = w_raw[u].rearrange("p t (c i) -> p c t i", i=4)
+        def interleave(dst, u, on_vector):
+            dst = dst.rearrange("p (c i) t -> p c t i", i=4)
+            src = w_raw[u][:].rearrange("p t (c i) -> p c t i", i=4)
             if on_vector:
                 nc.vector.tensor_copy(dst, src)
             else:
                 nc.scalar.activation(dst, src, COPY)
 
-        def quantize(values, words, plane, c0, c1):
+        def quantize(values, codes, scales):
             nc.vector.quantize_mx(
-                out=words[:, c0:c1].bitcast(FP8X4),
-                scales=plane[:, c0:c1],
-                in_=values[:, c0:c1, :].rearrange("p c t -> p (c t)"),
+                out=codes.bitcast(FP8X4), scales=scales, in_=values.rearrange("p c t -> p (c t)")
             )
 
-        third_in = keep.tile([P, P, PACK], BF16, name="third_in", align_bytes=64)
-        w_in.append(third_in[:])
-        for u in range(3):
-            interleave(u, False)
-        quantize(grouped, codes, scales, 0, 2 * P)
-        high_codes = keep.tile([P, 2 * P], U32, name="high_codes", tag="w_raw0", align_bytes=64)
-        high_scales = keep.tile([P, 2 * P], U8, name="high_scales", align_bytes=64)
-        for c0 in (P, 0):
-            quantize(high_in, high_codes, high_scales, c0, c0 + P)
-        quantize(grouped, codes, scales, 2 * P, 4 * P)
-        quantize(third_in, late_codes, late_scales, 0, P)
-        fourth_in = keep.tile([P, 2 * P, PACK], BF16, name="fourth_in", tag="w_raw2", align_bytes=64)
-        w_in.append(fourth_in[:, P:, :])
-        interleave(3, True)
-        quantize(fourth_in, late_codes, late_scales, P, 2 * P)
+        def operand(name, width, tag):
+            codes = keep.tile([P, width], U32, name="codes_" + name, tag=tag, align_bytes=64)
+            scales = keep.tile([P, width], U8, name="scales_" + name, align_bytes=64)
+            return codes, scales
+
+        w_in = [keep.tile([P, P, PACK], BF16, name="w_in%d" % u, align_bytes=64) for u in range(1, 3)]
+        interleave(grouped[:, 0:P, :], 0, False)
+        for u in range(1, 3):
+            interleave(w_in[u - 1][:], u, False)
+        first = operand("first", 2 * P, "codes_first")
+        quantize(grouped[:, 0 : 2 * P, :], first[0][:], first[1][:])
+        rest = operand("rest", G - P, "w_raw0")
+        for c in (1, 3, 2):
+            cols = slice((c - 1) * P, c * P)
+            quantize(grouped[:, (c + 1) * P : (c + 2) * P, :], rest[0][:, cols], rest[1][:, cols])
+        w_mx = [(first[0][:, 0:P], first[1][:, 0:P])]
+        for u in range(1, TILES):
+            if u == TILES - 1:
+                w_in.append(keep.tile([P, P, PACK], BF16, name="w_in3", tag="w_raw2", align_bytes=64))
+                interleave(w_in[u - 1][:], u, True)
+            codes, scales = operand("w%d" % u, P, "codes_w%d" % u)
+            quantize(w_in[u - 1][:], codes[:], scales[:])
+            w_mx.append((codes[:], scales[:]))
 
         result = keep.tile([P, 2, G], F32, name="result")
-        reused = keep.tile([P, TILES - 1, G], F32, name="reused", tag="w_raw2", align_bytes=64)
-
-        def staged(u, g0, g1):
-            if u > 1 or u == 1 and g0 >= 2 * P:
-                return reused[:, u - 1, g0:g1]
-            return result[:, u, g0:g1]
-
+        reused = keep.tile([P, 2, G], F32, name="reused", tag="w_raw2", align_bytes=64)
+        staged = [result[:, 0, :], result[:, 1, :], reused[:, 0, :], reused[:, 1, :]]
         out_rows = out.rearrange("(u p) g -> p u g", p=P)
 
         def part(u, cuts, on_vector):
             acc = psum.tile([P, 512], F32, name="acc")
-            first, end = cuts[0], cuts[-1]
+            start, end = cuts[0], cuts[-1]
             for g0, g1 in zip(cuts, cuts[1:]):
-                if g0 < 2 * P:
-                    moving = (codes[:, P + g0 : P + g1], scales[:, P + g0 : P + g1])
+                if g0 < P:
+                    moving = (first[0][:, P + g0 : P + g1], first[1][:, P + g0 : P + g1])
                 else:
-                    moving = (high_codes[:, g0 - 2 * P : g1 - 2 * P], high_scales[:, g0 - 2 * P : g1 - 2 * P])
+                    moving = (rest[0][:, g0 - P : g1 - P], rest[1][:, g0 - P : g1 - P])
                 nc.tensor.matmul_mx(
-                    out=acc[:, g0 - first : g1 - first],
+                    out=acc[:, g0 - start : g1 - start],
                     lhsT=w_mx[u][0].bitcast(FP8X4),
                     lhsT_scale=w_mx[u][1],
                     rhs=moving[0].bitcast(FP8X4),
@@ -153,27 +145,24 @@ def tile_attend_bag_bias_kernel(tc, xT, w, bias, offs, out):
                     start=True,
                     stop=True,
                 )
-            dst, src, b = staged(u, first, end), acc[:, 0 : end - first], bias_cols[:, u : u + 1]
+            dst, src, b = staged[u][:, start:end], acc[:, 0 : end - start], bias_cols[:, u : u + 1]
             if on_vector:
                 nc.vector.tensor_scalar(dst, src, b, None, ADD)
             else:
                 nc.scalar.activation(dst, src, IDENTITY, bias=b)
 
         def store(u, g0, g1):
-            nc.sync.dma_start(out_rows[:, u, g0:g1], staged(u, g0, g1))
+            nc.sync.dma_start(out_rows[:, u, g0:g1], staged[u][:, g0:g1])
 
-        part(0, (0, P), False)
-        store(0, 0, P)
-        part(0, (3 * P, G), False)
-        part(0, (2 * P, 3 * P), False)
-        store(0, 2 * P, G)
-        part(0, (P, 2 * P), False)
-        store(0, P, 2 * P)
-        for h in range(2):
-            part(1, (2 * P * h, 2 * P * (h + 1)), h == 1)
-            store(1, 2 * P * h, 2 * P * (h + 1))
+        for chunks in ((0, 1), (3, 2)):
+            for c in chunks:
+                part(0, (c * P, (c + 1) * P), False)
+            store(0, min(chunks) * P, (max(chunks) + 1) * P)
+        for cuts in ((0, P, 2 * P), (2 * P, G)):
+            part(1, cuts, False)
+            store(1, cuts[0], cuts[-1])
         for u in range(2, TILES):
-            part(u, (0, 2 * P), False)
+            part(u, (0, P, 2 * P), False)
             part(u, (2 * P, 3 * P), True)
-            part(u, (3 * P, G), u == 2)
+            part(u, (3 * P, G), True)
             store(u, 0, G)

@@ -1,7 +1,6 @@
 from contextlib import ExitStack
 
 import concourse.mybir as mybir
-from concourse.masks import make_identity
 
 D, T, G, BAG, M = 512, 4096, 512, 2, 512
 FLOPS = 2 * D * M * G
@@ -19,6 +18,8 @@ IDENTITY = mybir.ActivationFunctionType.Identity
 P = 128
 PACK = 4
 TILES = M // P
+QUAD = 32
+SPLIT = 304
 
 
 def tile_attend_bag_bias_kernel(tc, xT, w, bias, offs, out):
@@ -28,15 +29,18 @@ def tile_attend_bag_bias_kernel(tc, xT, w, bias, offs, out):
         psum = ctx.enter_context(tc.psum_pool(name="psum", bufs=8))
 
         offsets = keep.tile([P, G * BAG // 16], U16, name="offsets")
-        bias_rows = keep.tile([P, P], F32, name="bias_rows")
-        nc.vector.memset(bias_rows[:], 0.0)
+        bias_rows = keep.tile([P, P], F32, name="bias_rows", align_bytes=64)
+        nc.gpsimd.memset(bias_rows[:], 0.0)
         pair = keep.tile([P, 2 * T], F32, name="pair")
         planes = [pair[:, 0:T], pair[:, T:]]
         planes.extend(keep.tile([P, T], F32, name="plane%d" % t)[:] for t in range(2, PACK))
         x_rows = xT.rearrange("(p t) c -> p t c", t=PACK)
         w_rows = w.rearrange("(p t) m -> p t m", t=PACK)
         nc.sync.dma_start(pair[:], xT.rearrange("(p h t) c -> p h (t c)", h=2, t=2)[:, 0, :])
-        nc.sync.dma_start(bias_rows[0:TILES, :], bias.rearrange("(u p) o -> u (p o)", p=P))
+        nc.sync.dma_start(
+            bias_rows[0:P:QUAD, :].rearrange("q (u c) -> q u c", c=QUAD),
+            bias.rearrange("(u q c) o -> q u (c o)", u=TILES, c=QUAD),
+        )
         nc.sync.dma_start(offsets[:], offs)
         for t in range(2, PACK):
             nc.sync.dma_start(planes[t], x_rows[:, t, :])
@@ -46,12 +50,10 @@ def tile_attend_bag_bias_kernel(tc, xT, w, bias, offs, out):
             nc.sync.dma_start(raw[:], w_rows[:, :, u * P : (u + 1) * P])
             w_raw.append(raw)
 
-        ident = keep.tile([P, P], F32, name="ident")
-        make_identity(nc, ident[:])
-        turned = psum.tile([P, 512], F32, name="acc")
-        nc.tensor.transpose(turned[:, 0:P], bias_rows[:], ident[:])
+        turned = keep.tile([P, P], F32, name="turned", align_bytes=64)
+        nc.vector.transpose(turned[:], bias_rows[:])
         bias_cols = keep.tile([P, TILES], F32, name="bias_cols")
-        nc.scalar.activation(bias_cols[:], turned[:, 0:TILES], IDENTITY)
+        nc.scalar.activation(bias_cols[:], turned[:, 0:P:QUAD], IDENTITY)
 
         grouped = keep.tile([P, P + G, PACK], BF16, name="grouped", align_bytes=64)
 
@@ -63,10 +65,10 @@ def tile_attend_bag_bias_kernel(tc, xT, w, bias, offs, out):
             else:
                 nc.scalar.activation(dst, window, COPY)
 
-        def add(picked, t, c):
-            pairs = picked[:, c * P * BAG : (c + 1) * P * BAG].rearrange("p (g j) -> p g j", j=BAG)
-            dst = grouped[:, (c + 1) * P : (c + 2) * P, t]
-            if c % 2 == 1:
+        def add(on_vector, picked, t, g0, g1):
+            pairs = picked[:, g0 * BAG : g1 * BAG].rearrange("p (g j) -> p g j", j=BAG)
+            dst = grouped[:, P + g0 : P + g1, t]
+            if on_vector:
                 with nc.allow_low_precision(reason="summed in float32, rounded once"):
                     nc.vector.tensor_reduce(dst, pairs, mybir.AxisListType.X, ADD)
             else:
@@ -75,16 +77,21 @@ def tile_attend_bag_bias_kernel(tc, xT, w, bias, offs, out):
         last = PACK - 1
         for t in range(last):
             picked = keep.tile([P, G * BAG], F32 if t < 2 else BF16, name="picked%d" % t)
-            for h in range(2):
-                gather(t < 2, picked, t, 2 * P * h, 2 * P * (h + 1))
-                for c in range(2 * h, 2 * h + 2):
-                    add(picked, t, c)
-        wide = keep.tile([P, G * BAG], F32, name="wide")
-        narrow = keep.tile([P, G * BAG], BF16, name="narrow")
-        for c in range(4):
-            gather(c % 2 == 0, narrow if c % 2 else wide, last, c * P, (c + 1) * P)
-        for c in range(4):
-            add(narrow if c % 2 else wide, last, c)
+            gather(t < 2, picked, t, 0, 2 * P)
+            add(False, picked, t, 0, 2 * P)
+            gather(t < 2, picked, t, 2 * P, G)
+            add(False, picked, t, 2 * P, SPLIT)
+            add(True, picked, t, SPLIT, G)
+        picked = keep.tile([P, G * BAG], BF16, name="picked3")
+        for on_vector, g0, g1 in (
+            (True, 0, 96),
+            (False, 96, 192),
+            (True, 192, 368),
+            (False, 368, G),
+        ):
+            gather(on_vector, picked, last, g0, g1)
+        for g0, g1 in ((0, 192), (192, SPLIT), (368, G), (SPLIT, 368)):
+            add(g0 >= SPLIT, picked, last, g0, g1)
 
         def interleave(dst, u, on_vector):
             dst = dst.rearrange("p (c i) t -> p c t i", i=4)
@@ -111,9 +118,9 @@ def tile_attend_bag_bias_kernel(tc, xT, w, bias, offs, out):
         first = operand("first", 2 * P, "codes_first")
         quantize(grouped[:, 0 : 2 * P, :], first[0][:], first[1][:])
         rest = operand("rest", G - P, "w_raw0")
-        for c in (1, 3, 2):
-            cols = slice((c - 1) * P, c * P)
-            quantize(grouped[:, (c + 1) * P : (c + 2) * P, :], rest[0][:, cols], rest[1][:, cols])
+        for g0, g1 in ((P, 2 * P), (2 * P, 3 * P), (3 * P, G)):
+            cols = slice(g0 - P, g1 - P)
+            quantize(grouped[:, P + g0 : P + g1, :], rest[0][:, cols], rest[1][:, cols])
         w_mx = [(first[0][:, 0:P], first[1][:, 0:P])]
         for u in range(1, TILES):
             if u == TILES - 1:
@@ -145,7 +152,8 @@ def tile_attend_bag_bias_kernel(tc, xT, w, bias, offs, out):
                     start=True,
                     stop=True,
                 )
-            dst, src, b = staged[u][:, start:end], acc[:, 0 : end - start], bias_cols[:, u : u + 1]
+            dst, src = staged[u][:, start:end], acc[:, 0 : end - start]
+            b = bias_cols[:, u : u + 1]
             if on_vector:
                 nc.vector.tensor_scalar(dst, src, b, None, ADD)
             else:
@@ -154,10 +162,10 @@ def tile_attend_bag_bias_kernel(tc, xT, w, bias, offs, out):
         def store(u, g0, g1):
             nc.sync.dma_start(out_rows[:, u, g0:g1], staged[u][:, g0:g1])
 
-        for chunks in ((0, 1), (3, 2)):
-            for c in chunks:
+        for h in range(2):
+            for c in range(2 * h, 2 * h + 2):
                 part(0, (c * P, (c + 1) * P), False)
-            store(0, min(chunks) * P, (max(chunks) + 1) * P)
+            store(0, 2 * P * h, 2 * P * (h + 1))
         for cuts in ((0, P, 2 * P), (2 * P, G)):
             part(1, cuts, False)
             store(1, cuts[0], cuts[-1])

@@ -19,7 +19,6 @@ P = 128
 PACK = 4
 TILES = M // P
 QUAD = 32
-SPLIT = 304
 
 
 def tile_attend_bag_bias_kernel(tc, xT, w, bias, offs, out):
@@ -77,21 +76,15 @@ def tile_attend_bag_bias_kernel(tc, xT, w, bias, offs, out):
         last = PACK - 1
         for t in range(last):
             picked = keep.tile([P, G * BAG], F32 if t < 2 else BF16, name="picked%d" % t)
-            gather(t < 2, picked, t, 0, 2 * P)
-            add(False, picked, t, 0, 2 * P)
-            gather(t < 2, picked, t, 2 * P, G)
-            add(False, picked, t, 2 * P, SPLIT)
-            add(True, picked, t, SPLIT, G)
+            for h in range(2):
+                gather(t < 2, picked, t, 2 * P * h, 2 * P * (h + 1))
+                for c in range(2 * h, 2 * h + 2):
+                    add(c in (0, 3), picked, t, c * P, (c + 1) * P)
         picked = keep.tile([P, G * BAG], BF16, name="picked3")
-        for on_vector, g0, g1 in (
-            (True, 0, 96),
-            (False, 96, 192),
-            (True, 192, 368),
-            (False, 368, G),
-        ):
-            gather(on_vector, picked, last, g0, g1)
-        for g0, g1 in ((0, 192), (192, SPLIT), (368, G), (SPLIT, 368)):
-            add(g0 >= SPLIT, picked, last, g0, g1)
+        for c in (1, 0, 2, 3):
+            gather(c in (1, 2), picked, last, c * P, (c + 1) * P)
+        for c in (1, 0, 2, 3):
+            add(c in (0, 3), picked, last, c * P, (c + 1) * P)
 
         def interleave(dst, u, on_vector):
             dst = dst.rearrange("p (c i) t -> p c t i", i=4)

@@ -8,6 +8,7 @@ FLOPS = 2 * D * M * G
 F32 = mybir.dt.float32
 BF16 = mybir.dt.bfloat16
 U32 = mybir.dt.uint32
+I32 = mybir.dt.int32
 U16 = mybir.dt.uint16
 U8 = mybir.dt.uint8
 FP8X4 = mybir.dt.float8_e4m3fn_x4
@@ -43,12 +44,6 @@ def tile_attend_bag_bias_kernel(tc, xT, w, bias, offs, out):
         nc.sync.dma_start(offsets[:], offs)
         for t in range(2, PACK):
             nc.sync.dma_start(planes[t], x_rows[:, t, :])
-        w_raw = []
-        for u in range(TILES):
-            raw = keep.tile([P, PACK, P], F32, name="w_raw%d" % u, align_bytes=64)
-            nc.sync.dma_start(raw[:], w_rows[:, :, u * P : (u + 1) * P])
-            w_raw.append(raw)
-
         turned = keep.tile([P, P], F32, name="turned", align_bytes=64)
         nc.vector.transpose(turned[:], bias_rows[:])
         bias_cols = keep.tile([P, TILES], F32, name="bias_cols")
@@ -80,6 +75,28 @@ def tile_attend_bag_bias_kernel(tc, xT, w, bias, offs, out):
                 gather(t < 2, picked, t, 2 * P * h, 2 * P * (h + 1))
                 for c in range(2 * h, 2 * h + 2):
                     add(c in (0, 3), picked, t, c * P, (c + 1) * P)
+        warm_codes = keep.tile([P, P], U32, name="warm_codes", align_bytes=64)
+        warm_scales = keep.tile([P, P], U8, name="warm_scales", align_bytes=64)
+        warm_cue = keep.tile([P, QUAD], U32, name="warm_cue", align_bytes=64)
+        nc.vector.quantize_mx(out=warm_codes[:].bitcast(FP8X4), scales=warm_scales[:], in_=picked[:, 0 : PACK * P])
+        w_raw = []
+        for u in range(TILES):
+            raw = keep.tile([P, PACK, P], F32, name="w_raw%d" % u, align_bytes=64)
+            nc.sync.dma_start(raw[:], w_rows[:, :, u * P : (u + 1) * P])
+            w_raw.append(raw)
+            if u == 1:
+                nc.sync.dma_start(warm_cue[:].bitcast(I32), warm_codes[:, 0:QUAD].bitcast(I32))
+        warm = psum.tile([P, 512], F32, name="acc")
+        for k in range(6):
+            nc.tensor.matmul_mx(
+                out=warm[0:QUAD, (k % 4) * P : (k % 4 + 1) * P],
+                lhsT=warm_cue[:].bitcast(FP8X4),
+                lhsT_scale=warm_scales[:, 0:QUAD],
+                rhs=warm_codes[:].bitcast(FP8X4),
+                rhs_scale=warm_scales[:],
+                start=True,
+                stop=True,
+            )
         picked = keep.tile([P, G * BAG], BF16, name="picked3")
         for c in (1, 0, 2, 3):
             gather(c in (1, 2), picked, last, c * P, (c + 1) * P)

@@ -132,17 +132,8 @@ def tile_attend_bag_bias_kernel(tc, xT, w, bias, offs, out):
             cols = slice(g0 - P, g1 - P)
             quantize(grouped[:, P + g0 : P + g1, :], rest[0][:, cols], rest[1][:, cols])
         w_mx = [(first[0][:, 0:P], first[1][:, 0:P])]
-        for u in range(1, TILES):
-            if u == TILES - 1:
-                w_in.append(keep.tile([P, P, PACK], BF16, name="w_in3", tag="w_raw2", align_bytes=64))
-                interleave(w_in[u - 1][:], u, True)
-            codes, scales = operand("w%d" % u, P, "codes_w%d" % u)
-            quantize(w_in[u - 1][:], codes[:], scales[:])
-            w_mx.append((codes[:], scales[:]))
-
         result = keep.tile([P, 2, G], F32, name="result")
-        reused = keep.tile([P, 2, G], F32, name="reused", tag="w_raw2", align_bytes=64)
-        staged = [result[:, 0, :], result[:, 1, :], reused[:, 0, :], reused[:, 1, :]]
+        staged = [result[:, 0, :], result[:, 1, :]]
         out_rows = out.rearrange("(u p) g -> p u g", p=P)
 
         def part(u, cuts, on_vector):
@@ -172,10 +163,24 @@ def tile_attend_bag_bias_kernel(tc, xT, w, bias, offs, out):
         def store(u, g0, g1):
             nc.sync.dma_start(out_rows[:, u, g0:g1], staged[u][:, g0:g1])
 
-        for h in range(2):
-            for c in range(2 * h, 2 * h + 2):
-                part(0, (c * P, (c + 1) * P), False)
-            store(0, 2 * P * h, 2 * P * (h + 1))
+        def quantize_w(u):
+            codes, scales = operand("w%d" % u, P, "codes_w%d" % u)
+            quantize(w_in[u - 1][:], codes[:], scales[:])
+            w_mx.append((codes[:], scales[:]))
+
+        quantize_w(1)
+        part(0, (0, P), True)
+        w_in.append(keep.tile([P, P, PACK], BF16, name="w_in3", tag="grouped", align_bytes=64))
+        interleave(w_in[2][:], 3, True)
+        quantize_w(2)
+        quantize_w(3)
+        reused = keep.tile([P, 2, G], F32, name="reused", tag="grouped", align_bytes=64)
+        staged.extend([reused[:, 0, :], reused[:, 1, :]])
+        part(0, (P, 2 * P), False)
+        store(0, 0, 2 * P)
+        for c in (2, 3):
+            part(0, (c * P, (c + 1) * P), False)
+        store(0, 2 * P, G)
         for cuts in ((0, P, 2 * P), (2 * P, G)):
             part(1, cuts, False)
             store(1, cuts[0], cuts[-1])

@@ -29,25 +29,17 @@ def tile_attend_bag_bias_kernel(tc, xT, w, bias, offs, out):
         psum = ctx.enter_context(tc.psum_pool(name="psum", bufs=8))
 
         offsets = keep.tile([P, G * BAG // 16], U16, name="offsets")
-        bias_rows = keep.tile([P, P], F32, name="bias_rows", align_bytes=64)
-        nc.gpsimd.memset(bias_rows[:], 0.0)
         pair = keep.tile([P, 2 * T], F32, name="pair")
         planes = [pair[:, 0:T], pair[:, T:]]
         planes.extend(keep.tile([P, T], F32, name="plane%d" % t)[:] for t in range(2, PACK))
         x_rows = xT.rearrange("(p t) c -> p t c", t=PACK)
         w_rows = w.rearrange("(p t) m -> p t m", t=PACK)
         nc.sync.dma_start(pair[:], xT.rearrange("(p h t) c -> p h (t c)", h=2, t=2)[:, 0, :])
-        nc.sync.dma_start(
-            bias_rows[0:P:QUAD, :].rearrange("q (u c) -> q u c", c=QUAD),
-            bias.rearrange("(u q c) o -> q u (c o)", u=TILES, c=QUAD),
-        )
         nc.sync.dma_start(offsets[:], offs)
         for t in range(2, PACK):
             nc.sync.dma_start(planes[t], x_rows[:, t, :])
-        turned = keep.tile([P, P], F32, name="turned", align_bytes=64)
-        nc.vector.transpose(turned[:], bias_rows[:])
-        bias_cols = keep.tile([P, TILES], F32, name="bias_cols")
-        nc.scalar.activation(bias_cols[:], turned[:, 0:P:QUAD], IDENTITY)
+        bias_cols = keep.tile([P, TILES, 8], F32, name="bias_cols")
+        early = keep.tile([P, 2, P], BF16, name="early")
 
         grouped = keep.tile([P, P + G, PACK], BF16, name="grouped", align_bytes=64)
 
@@ -61,7 +53,7 @@ def tile_attend_bag_bias_kernel(tc, xT, w, bias, offs, out):
 
         def add(on_vector, picked, t, g0, g1):
             pairs = picked[:, g0 * BAG : g1 * BAG].rearrange("p (g j) -> p g j", j=BAG)
-            dst = grouped[:, P + g0 : P + g1, t]
+            dst = early[:, t, :] if g0 == 0 and t < 2 else grouped[:, P + g0 : P + g1, t]
             if on_vector:
                 with nc.allow_low_precision(reason="summed in float32, rounded once"):
                     nc.vector.tensor_reduce(dst, pairs, mybir.AxisListType.X, ADD)
@@ -69,12 +61,21 @@ def tile_attend_bag_bias_kernel(tc, xT, w, bias, offs, out):
                 nc.gpsimd.tensor_tensor(out=dst, in0=pairs[:, :, 0], in1=pairs[:, :, 1], op=ADD)
 
         last = PACK - 1
-        for t in range(last):
-            picked = keep.tile([P, G * BAG], F32 if t < 2 else BF16, name="picked%d" % t)
-            for h in range(2):
-                gather(t < 2, picked, t, 2 * P * h, 2 * P * (h + 1))
-                for c in range(2 * h, 2 * h + 2):
-                    add(c in (0, 3), picked, t, c * P, (c + 1) * P)
+
+        def gather_and_add(picked, t, h):
+            gather(t < 2, picked, t, 2 * P * h, 2 * P * (h + 1))
+            for c in range(2 * h, 2 * h + 2):
+                add(c in (0, 3), picked, t, c * P, (c + 1) * P)
+
+        for h in range(2):
+            for t in range(2):
+                picked = keep.tile([P, G * BAG], F32, name="picked%d%d" % (t, h))
+                gather_and_add(picked, t, h)
+            if h == 0:
+                nc.scalar.activation(grouped[:, P : 2 * P, 0:2], early[:].rearrange("p t g -> p g t"), COPY)
+        picked = keep.tile([P, G * BAG], BF16, name="picked2")
+        for h in range(2):
+            gather_and_add(picked, 2, h)
         warm_codes = keep.tile([P, P], U32, name="warm_codes", align_bytes=64)
         warm_scales = keep.tile([P, P], U8, name="warm_scales", align_bytes=64)
         warm_cue = keep.tile([P, QUAD], U32, name="warm_cue", align_bytes=64)
@@ -86,6 +87,9 @@ def tile_attend_bag_bias_kernel(tc, xT, w, bias, offs, out):
             w_raw.append(raw)
             if u == 1:
                 nc.sync.dma_start(warm_cue[:].bitcast(I32), warm_codes[:, 0:QUAD].bitcast(I32))
+            if u == 2:
+                with nc.allow_non_contiguous_dma(reason="one bias value a partition and tile"):
+                    nc.sync.dma_start(bias_cols[:, :, 0:1], bias.rearrange("(u p) o -> p u o", p=P))
         warm = psum.tile([P, 512], F32, name="acc")
         for k in range(6):
             nc.tensor.matmul_mx(
@@ -154,7 +158,7 @@ def tile_attend_bag_bias_kernel(tc, xT, w, bias, offs, out):
                     stop=True,
                 )
             dst, src = staged[u][:, start:end], acc[:, 0 : end - start]
-            b = bias_cols[:, u : u + 1]
+            b = bias_cols[:, u, 0:1]
             if on_vector:
                 nc.vector.tensor_scalar(dst, src, b, None, ADD)
             else:

@@ -67,10 +67,10 @@ def tile_attend_bag_bias_kernel(tc, xT, w, bias, offs, out):
             for c in range(2 * h, 2 * h + 2):
                 add(c in (0, 3), picked, t, c * P, (c + 1) * P)
 
+        early_picked = [keep.tile([P, G * BAG], F32, name="picked%d" % t) for t in range(2)]
         for h in range(2):
             for t in range(2):
-                picked = keep.tile([P, G * BAG], F32, name="picked%d%d" % (t, h))
-                gather_and_add(picked, t, h)
+                gather_and_add(early_picked[t], t, h)
             if h == 0:
                 nc.scalar.activation(grouped[:, P : 2 * P, 0:2], early[:].rearrange("p t g -> p g t"), COPY)
         picked = keep.tile([P, G * BAG], BF16, name="picked2")
@@ -101,7 +101,7 @@ def tile_attend_bag_bias_kernel(tc, xT, w, bias, offs, out):
                 start=True,
                 stop=True,
             )
-        picked = keep.tile([P, G * BAG], BF16, name="picked3")
+        picked = keep.tile([P, G * BAG], F32, name="picked3")
         for c in (1, 0, 2, 3):
             gather(c in (1, 2), picked, last, c * P, (c + 1) * P)
         for c in (1, 0, 2, 3):

from contextlib import ExitStack

import concourse.mybir as mybir

D, T, G, BAG, M = 512, 4096, 512, 2, 512
FLOPS = 2 * D * M * G

F32 = mybir.dt.float32
BF16 = mybir.dt.bfloat16
U32 = mybir.dt.uint32
I32 = mybir.dt.int32
U16 = mybir.dt.uint16
U8 = mybir.dt.uint8
FP8X4 = mybir.dt.float8_e4m3fn_x4
ADD = mybir.AluOpType.add
COPY = mybir.ActivationFunctionType.Copy
IDENTITY = mybir.ActivationFunctionType.Identity

P = 128
PACK = 4
TILES = M // P
QUAD = 32


def tile_attend_bag_bias_kernel(tc, xT, w, bias, offs, out):
    nc = tc.nc
    with ExitStack() as ctx:
        keep = ctx.enter_context(tc.tile_pool(name="keep", bufs=1))
        psum = ctx.enter_context(tc.psum_pool(name="psum", bufs=8))

        offsets = keep.tile([P, G * BAG // 16], U16, name="offsets")
        pair = keep.tile([P, 2 * T], F32, name="pair")
        planes = [pair[:, 0:T], pair[:, T:]]
        planes.extend(keep.tile([P, T], F32, name="plane%d" % t)[:] for t in range(2, PACK))
        x_rows = xT.rearrange("(p t) c -> p t c", t=PACK)
        w_rows = w.rearrange("(p t) m -> p t m", t=PACK)
        nc.sync.dma_start(pair[:], xT.rearrange("(p h t) c -> p h (t c)", h=2, t=2)[:, 0, :])
        nc.sync.dma_start(offsets[:], offs)
        for t in range(2, PACK):
            nc.sync.dma_start(planes[t], x_rows[:, t, :])
        bias_cols = keep.tile([P, TILES, 8], F32, name="bias_cols")
        early = keep.tile([P, 2, P], BF16, name="early")

        grouped = keep.tile([P, P + G, PACK], BF16, name="grouped", align_bytes=64)

        def gather(on_vector, picked, t, g0, g1):
            window = planes[t].indirect(offsets[:, g0 * BAG // 16 : g1 * BAG // 16])
            dst = picked[:, g0 * BAG : g1 * BAG]
            if on_vector:
                nc.vector.tensor_copy(dst, window)
            else:
                nc.scalar.activation(dst, window, COPY)

        def add(on_vector, picked, t, g0, g1):
            pairs = picked[:, g0 * BAG : g1 * BAG].rearrange("p (g j) -> p g j", j=BAG)
            dst = early[:, t, :] if g0 == 0 and t < 2 else grouped[:, P + g0 : P + g1, t]
            if on_vector:
                with nc.allow_low_precision(reason="summed in float32, rounded once"):
                    nc.vector.tensor_reduce(dst, pairs, mybir.AxisListType.X, ADD)
            else:
                nc.gpsimd.tensor_tensor(out=dst, in0=pairs[:, :, 0], in1=pairs[:, :, 1], op=ADD)

        last = PACK - 1

        def gather_and_add(picked, t, h):
            gather(t < 2, picked, t, 2 * P * h, 2 * P * (h + 1))
            for c in range(2 * h, 2 * h + 2):
                add(c in (0, 3), picked, t, c * P, (c + 1) * P)

        early_picked = [keep.tile([P, G * BAG], F32, name="picked%d" % t) for t in range(2)]
        for h in range(2):
            for t in range(2):
                gather_and_add(early_picked[t], t, h)
            if h == 0:
                nc.scalar.activation(grouped[:, P : 2 * P, 0:2], early[:].rearrange("p t g -> p g t"), COPY)
        picked = keep.tile([P, G * BAG], BF16, name="picked2")
        for h in range(2):
            gather_and_add(picked, 2, h)
        warm_codes = keep.tile([P, P], U32, name="warm_codes", align_bytes=64)
        warm_scales = keep.tile([P, P], U8, name="warm_scales", align_bytes=64)
        warm_cue = keep.tile([P, QUAD], U32, name="warm_cue", align_bytes=64)
        nc.vector.quantize_mx(out=warm_codes[:].bitcast(FP8X4), scales=warm_scales[:], in_=picked[:, 0 : PACK * P])
        w_raw = []
        for u in range(TILES):
            raw = keep.tile([P, PACK, P], F32, name="w_raw%d" % u, align_bytes=64)
            nc.sync.dma_start(raw[:], w_rows[:, :, u * P : (u + 1) * P])
            w_raw.append(raw)
            if u == 1:
                nc.sync.dma_start(warm_cue[:].bitcast(I32), warm_codes[:, 0:QUAD].bitcast(I32))
            if u == 2:
                with nc.allow_non_contiguous_dma(reason="one bias value a partition and tile"):
                    nc.sync.dma_start(bias_cols[:, :, 0:1], bias.rearrange("(u p) o -> p u o", p=P))
        warm = psum.tile([P, 512], F32, name="acc")
        for k in range(6):
            nc.tensor.matmul_mx(
                out=warm[0:QUAD, (k % 4) * P : (k % 4 + 1) * P],
                lhsT=warm_cue[:].bitcast(FP8X4),
                lhsT_scale=warm_scales[:, 0:QUAD],
                rhs=warm_codes[:].bitcast(FP8X4),
                rhs_scale=warm_scales[:],
                start=True,
                stop=True,
            )
        picked = keep.tile([P, G * BAG], F32, name="picked3")
        for c in (1, 0, 2, 3):
            gather(c in (1, 2), picked, last, c * P, (c + 1) * P)
        for c in (1, 0, 2, 3):
            add(c in (0, 3), picked, last, c * P, (c + 1) * P)

        def interleave(dst, u, on_vector):
            dst = dst.rearrange("p (c i) t -> p c t i", i=4)
            src = w_raw[u][:].rearrange("p t (c i) -> p c t i", i=4)
            if on_vector:
                nc.vector.tensor_copy(dst, src)
            else:
                nc.scalar.activation(dst, src, COPY)

        def quantize(values, codes, scales):
            nc.vector.quantize_mx(
                out=codes.bitcast(FP8X4), scales=scales, in_=values.rearrange("p c t -> p (c t)")
            )

        def operand(name, width, tag):
            codes = keep.tile([P, width], U32, name="codes_" + name, tag=tag, align_bytes=64)
            scales = keep.tile([P, width], U8, name="scales_" + name, align_bytes=64)
            return codes, scales

        w_in = [keep.tile([P, P, PACK], BF16, name="w_in%d" % u, align_bytes=64) for u in range(1, 3)]
        interleave(grouped[:, 0:P, :], 0, False)
        for u in range(1, 3):
            interleave(w_in[u - 1][:], u, False)
        first = operand("first", 2 * P, "codes_first")
        quantize(grouped[:, 0 : 2 * P, :], first[0][:], first[1][:])
        rest = operand("rest", G - P, "w_raw0")
        for g0, g1 in ((P, 2 * P), (2 * P, 3 * P), (3 * P, G)):
            cols = slice(g0 - P, g1 - P)
            quantize(grouped[:, P + g0 : P + g1, :], rest[0][:, cols], rest[1][:, cols])
        w_mx = [(first[0][:, 0:P], first[1][:, 0:P])]
        result = keep.tile([P, 2, G], F32, name="result")
        staged = [result[:, 0, :], result[:, 1, :]]
        out_rows = out.rearrange("(u p) g -> p u g", p=P)

        def part(u, cuts, on_vector):
            acc = psum.tile([P, 512], F32, name="acc")
            start, end = cuts[0], cuts[-1]
            for g0, g1 in zip(cuts, cuts[1:]):
                if g0 < P:
                    moving = (first[0][:, P + g0 : P + g1], first[1][:, P + g0 : P + g1])
                else:
                    moving = (rest[0][:, g0 - P : g1 - P], rest[1][:, g0 - P : g1 - P])
                nc.tensor.matmul_mx(
                    out=acc[:, g0 - start : g1 - start],
                    lhsT=w_mx[u][0].bitcast(FP8X4),
                    lhsT_scale=w_mx[u][1],
                    rhs=moving[0].bitcast(FP8X4),
                    rhs_scale=moving[1],
                    start=True,
                    stop=True,
                )
            dst, src = staged[u][:, start:end], acc[:, 0 : end - start]
            b = bias_cols[:, u, 0:1]
            if on_vector:
                nc.vector.tensor_scalar(dst, src, b, None, ADD)
            else:
                nc.scalar.activation(dst, src, IDENTITY, bias=b)

        def store(u, g0, g1):
            nc.sync.dma_start(out_rows[:, u, g0:g1], staged[u][:, g0:g1])

        def quantize_w(u):
            codes, scales = operand("w%d" % u, P, "codes_w%d" % u)
            quantize(w_in[u - 1][:], codes[:], scales[:])
            w_mx.append((codes[:], scales[:]))

        quantize_w(1)
        part(0, (0, P), True)
        w_in.append(keep.tile([P, P, PACK], BF16, name="w_in3", tag="grouped", align_bytes=64))
        interleave(w_in[2][:], 3, True)
        quantize_w(2)
        quantize_w(3)
        reused = keep.tile([P, 2, G], F32, name="reused", tag="grouped", align_bytes=64)
        staged.extend([reused[:, 0, :], reused[:, 1, :]])
        part(0, (P, 2 * P), False)
        store(0, 0, 2 * P)
        for c in (2, 3):
            part(0, (c * P, (c + 1) * P), False)
        store(0, 2 * P, G)
        for cuts in ((0, P, 2 * P), (2 * P, G)):
            part(1, cuts, False)
            store(1, cuts[0], cuts[-1])
        for u in range(2, TILES):
            part(u, (0, P, 2 * P), False)
            part(u, (2 * P, 3 * P), True)
            part(u, (3 * P, G), True)
            store(u, 0, G)
